import numpy as np
import ml_dtypes


def mxq(x, axis, fmt="e4m3"):
    dtype, down = {"e4m3": (ml_dtypes.float8_e4m3fn, 7), "e5m2": (ml_dtypes.float8_e5m2, 14)}[fmt]
    v = np.moveaxis(np.asarray(x, np.float32).astype(ml_dtypes.bfloat16).astype(np.float64), axis, -1)
    blocks = v.reshape(v.shape[:-1] + (-1, 32))
    amax = np.abs(blocks).max(-1, keepdims=True)
    byte = np.maximum(np.where(amax > 0, np.frexp(amax)[1] - 1 + 127, 0) - down, 1)
    scale = np.exp2(byte - 127.0)
    codes = (blocks / scale).astype(np.float32).astype(dtype).astype(np.float64)
    return np.moveaxis((codes * scale).reshape(v.shape), -1, axis)


WIDE = False


def mx_kscale(k):
    if not WIDE:
        return np.ones(k)
    levels = np.array([10, -10, 5, -5, 0])
    if k % 512:
        return np.exp2(np.random.permutation(np.resize(levels, k // 32))).repeat(32)
    a = np.empty((k // 512, 16))
    for p in range(k // 512):
        a[p, :8] = np.random.permutation(np.resize(levels, 8))
        for g in range(8):
            far = levels[np.abs(levels - a[p, g]) >= 10]
            a[p, g + 8] = far[np.random.randint(len(far))]
    return np.exp2(a.ravel()).repeat(32)


def f64(x):
    return np.asarray(x).astype(np.float64)


def striped(idx):
    return np.tile(idx.reshape(-1, 16).T, (8, 1)).astype(np.uint16)


def unstriped(offs):
    return offs[:16].T.reshape(-1).astype(np.int64)


def pack_weight(w):
    k, n = w.shape
    w = f64(np.asarray(w, np.float32).astype(ml_dtypes.bfloat16)).reshape(k // 32, 32, n)
    amax = np.abs(w).max(1)
    byte = np.clip(np.where(amax > 0, np.frexp(amax)[1] - 1 + 127 - 7, 1), 1, 254)
    scaled = (w * np.exp2(127.0 - byte)[:, None, :]).reshape(k, n).astype(np.float32)
    words = np.ascontiguousarray(scaled.reshape(k // 512, 128, 4, n).transpose(0, 1, 3, 2)).astype(ml_dtypes.float8_e4m3fn).view(np.uint8)
    return words, np.ascontiguousarray(byte.astype(np.uint8).reshape(k // 512, 16, n))


def unpack_weight(words, scales):
    g, p, n, _ = words.shape
    vals = np.ascontiguousarray(words).view(ml_dtypes.float8_e4m3fn).astype(np.float64) * np.repeat(np.exp2(scales.astype(np.float64) - 127.0), 8, axis=1)[..., None]
    return vals.transpose(0, 1, 3, 2).reshape(g * 512, n)


def relu(v):
    return np.maximum(v, 0.0)


K, T, D, S, V, N = 1024, 1024, 2, 512, 256, 128
P = 2 ** 7


def setup_inputs():
    n = np.random.standard_normal
    s = mx_kscale(K)[:, None]
    words, scales = pack_weight(n((K, N)) / np.sqrt(K) / s)
    return {
        "xT": (n((K, T)) * s / np.sqrt(D)).astype(ml_dtypes.bfloat16).astype(np.float32),
        "w_words": words,
        "w_scales": scales,
        "b": (0.3 * n((N, 1))).astype(np.float32),
        "gate": np.tile(np.random.uniform(0.5, 1.5, (D, 1, V)), (1, P, 1)).astype(ml_dtypes.bfloat16).astype(np.float32),
        "offs": striped(np.concatenate([np.random.permutation(T)[:V] for _ in range(D)])),
    }


def reference(xT, w_words, w_scales, b, gate, offs):
    w = unpack_weight(w_words, w_scales)
    idx = unstriped(offs)
    x = sum(f64(gate)[d, :1] * f64(xT)[:, idx[d * V:(d + 1) * V]] for d in range(D))
    return relu((w.T @ mxq(x, 0, "e4m3")) + f64(b))

@@ -1,0 +1,126 @@
+from contextlib import ExitStack
+
+import concourse.mybir as mybir
+
+K, T, D, V, N = 1024, 1024, 2, 256, 128
+S = D * V
+P = 128
+PACK = 4
+PASSES = K // (P * PACK)
+HALF = V // 2
+FLOPS = 2 * K * V * N
+
+F32 = mybir.dt.float32
+BF16 = mybir.dt.bfloat16
+I32 = mybir.dt.int32
+U32 = mybir.dt.uint32
+U16 = mybir.dt.uint16
+U8 = mybir.dt.uint8
+FP8X4 = mybir.dt.float8_e4m3fn_x4
+MULT = mybir.AluOpType.mult
+ADD = mybir.AluOpType.add
+RELU = mybir.ActivationFunctionType.Relu
+
+
+def tile_picked_bag_lin_relu_sub_l_kernel(tc, xT, w_words, w_scales, b, gate, offs, out):
+    nc = tc.nc
+    with ExitStack() as ctx:
+        keep = ctx.enter_context(tc.tile_pool(name="keep", bufs=1))
+        psum = ctx.enter_context(tc.psum_pool(name="psum", bufs=1))
+
+        offsets = keep.tile([P, S // 16], U16, name="offsets")
+        gates = keep.tile([P, S], F32, name="gates")
+        rows = [keep.tile([P, T], F32, name="rows%d" % i) for i in range(PASSES * PACK)]
+        w_codes = keep.tile([P, PASSES, N * PACK], U8, name="w_codes", align_bytes=64)
+        w_plane = keep.tile([P, PASSES, N], U8, name="w_plane", align_bytes=64)
+        bias = keep.tile([P, 1], F32, name="bias")
+        warm = keep.tile([P, 1], F32, name="warm")
+        warm_out = keep.tile([P, 1], F32, name="warm_out")
+        weighted = [keep.tile([P, PACK, S], F32, name="weighted%d" % a) for a in range(PASSES)]
+        sums = [keep.tile([P, V, PACK], BF16, name="sums%d" % a, align_bytes=64) for a in range(PASSES)]
+        x_codes = [keep.tile([P, V], U32, name="x_codes%d" % a, align_bytes=64) for a in range(PASSES)]
+        x_plane = [keep.tile([P, V], U8, name="x_plane%d" % a, align_bytes=64) for a in range(PASSES)]
+        acc = [psum.tile([P, HALF], F32, name="acc%d" % h) for h in range(2)]
+        result = [keep.tile([P, HALF], F32, name="result%d" % h) for h in range(2)]
+
+        x_rows = xT.rearrange("(a p t) c -> a t p c", a=PASSES, t=PACK)
+
+        nc.gpsimd.memset(w_plane[:].rearrange("p a m -> p (a m)").bitcast(U32), 0)
+        nc.gpsimd.memset(warm[:], 0.0)
+        nc.scalar.activation(warm_out[:], warm[:], RELU)
+
+        nc.sync.dma_start(offsets[:], offs)
+        nc.sync.dma_start(gates[:, 0:V], gate[0])
+        nc.sync.dma_start(rows[0][:], x_rows[0, 0])
+        nc.sync.dma_start(gates[:, V:S], gate[1])
+        for i in range(1, PASSES * PACK):
+            nc.sync.dma_start(rows[i][:], x_rows[i // PACK, i % PACK])
+        nc.sync.dma_start(w_codes[:].bitcast(I32), w_words.rearrange("a p m r -> p a (m r)").bitcast(I32))
+        for q in range(4):
+            nc.sync.dma_start(
+                w_plane[32 * q : 32 * q + 4, :, :].bitcast(I32),
+                w_scales[:, 4 * q : 4 * q + 4, :].rearrange("a q m -> q a m").bitcast(I32),
+            )
+        nc.sync.dma_start(bias[:], b)
+
+        def gather(i, first, count):
+            nc.vector.tensor_tensor(
+                weighted[i // PACK][:, i % PACK, first : first + count],
+                rows[i][:].indirect(offsets[:, first // 16 : (first + count) // 16]),
+                gates[:, first : first + count],
+                MULT,
+            )
+
+        def add(a, first, count):
+            nc.vector.tensor_tensor(
+                sums[a][:, first : first + count, :].rearrange("p (c i) t -> p c t i", i=2),
+                weighted[a][:, :, first : first + count].rearrange("p t (c i) -> p c t i", i=2),
+                weighted[a][:, :, V + first : V + first + count].rearrange("p t (c i) -> p c t i", i=2),
+                ADD,
+            )
+
+        def quantize(a, first, count):
+            nc.vector.quantize_mx(
+                out=x_codes[a][:, first : first + count].bitcast(FP8X4),
+                scales=x_plane[a][:, first : first + count],
+                in_=sums[a][:, first : first + count, :].rearrange("p v t -> p (v t)"),
+            )
+
+        def multiply(a, h):
+            cols = slice(h * HALF, (h + 1) * HALF)
+            nc.tensor.matmul_mx(
+                out=acc[h][:],
+                lhsT=w_codes[:, a, :].bitcast(FP8X4),
+                lhsT_scale=w_plane[:, a, :],
+                rhs=x_codes[a][:, cols].bitcast(FP8X4),
+                rhs_scale=x_plane[a][:, cols],
+                start=(a == 0),
+                stop=(a == PASSES - 1),
+            )
+
+        def finish(h):
+            nc.scalar.activation(result[h][:], acc[h][:], RELU, bias=bias[:])
+            nc.sync.dma_start(out[:, h * HALF : (h + 1) * HALF], result[h][:])
+
+        gather(0, 0, V)
+        gather(0, V, V)
+        for i in range(1, 5):
+            gather(i, 0, S)
+        add(0, 0, V)
+        gather(5, 0, S)
+        quantize(0, 0, V)
+        multiply(0, 0)
+        multiply(0, 1)
+        gather(6, 0, S)
+        gather(7, 0, HALF)
+        gather(7, V, HALF)
+        gather(7, HALF, HALF)
+        add(1, 0, HALF)
+        gather(7, V + HALF, HALF)
+        quantize(1, 0, HALF)
+        multiply(1, 0)
+        finish(0)
+        add(1, HALF, HALF)
+        quantize(1, HALF, HALF)
+        multiply(1, 1)
+        finish(1)

@@ -1,6 +1,7 @@
 from contextlib import ExitStack
 
 import concourse.mybir as mybir
+from concourse.masks import make_identity
 
 K, T, D, V, N = 1024, 1024, 2, 256, 128
 S = D * V
@@ -43,10 +44,18 @@ def tile_picked_bag_lin_relu_sub_l_kernel(tc, xT, w_words, w_scales, b, gate, of
         acc = [psum.tile([P, HALF], F32, name="acc%d" % h) for h in range(2)]
         result = [keep.tile([P, HALF], F32, name="result%d" % h) for h in range(2)]
 
+        ident_f32 = keep.tile([P, P], F32, name="ident_f32")
+        ident_bf16 = keep.tile([P, P], BF16, name="ident_bf16")
+        turned = [psum.tile([P, PACK, P], F32, name="turned%d" % h) for h in range(2)]
+        rounded = [keep.tile([P, PACK, P], BF16, name="rounded%d" % h) for h in range(2)]
+        back = [psum.tile([P, PACK, P], BF16, name="back%d" % h) for h in range(2)]
+
         x_rows = xT.rearrange("(a p t) c -> a t p c", a=PASSES, t=PACK)
 
         nc.gpsimd.memset(w_plane[:].rearrange("p a m -> p (a m)").bitcast(U32), 0)
         nc.gpsimd.memset(warm[:], 0.0)
+        make_identity(nc, ident_f32[:])
+        make_identity(nc, ident_bf16[:])
         nc.scalar.activation(warm_out[:], warm[:], RELU)
 
         nc.sync.dma_start(offsets[:], offs)
@@ -79,6 +88,27 @@ def tile_picked_bag_lin_relu_sub_l_kernel(tc, xT, w_words, w_scales, b, gate, of
                 ADD,
             )
 
+        def turn_and_sum(t):
+            for h in range(2):
+                for d in range(D):
+                    first = d * V + h * HALF
+                    nc.tensor.matmul(
+                        turned[h][:, t, :],
+                        weighted[0][:, t, first : first + HALF],
+                        ident_f32[:],
+                        start=(d == 0),
+                        stop=(d == D - 1),
+                        is_transpose=True,
+                    )
+
+        def turn_back(h):
+            nc.scalar.copy(rounded[h][:], turned[h][:])
+            for t in range(PACK):
+                nc.tensor.transpose(back[h][:, t, :], rounded[h][:, t, :], ident_bf16[:])
+
+        def interleave(h):
+            nc.scalar.copy(sums[0][:, h * HALF : (h + 1) * HALF, :], back[h][:].rearrange("p t v -> p v t"))
+
         def quantize(a, first, count):
             nc.vector.quantize_mx(
                 out=x_codes[a][:, first : first + count].bitcast(FP8X4),
@@ -104,14 +134,19 @@ def tile_picked_bag_lin_relu_sub_l_kernel(tc, xT, w_words, w_scales, b, gate, of
 
         gather(0, 0, V)
         gather(0, V, V)
-        for i in range(1, 5):
+        turn_and_sum(0)
+        for i in range(1, PACK):
             gather(i, 0, S)
-        add(0, 0, V)
-        gather(5, 0, S)
+            turn_and_sum(i)
+        for h in range(2):
+            turn_back(h)
+        for h in range(2):
+            interleave(h)
+        for i in range(PACK, 2 * PACK - 1):
+            gather(i, 0, S)
         quantize(0, 0, V)
         multiply(0, 0)
         multiply(0, 1)
-        gather(6, 0, S)
         gather(7, 0, HALF)
         gather(7, V, HALF)
         gather(7, HALF, HALF)

@@ -9,6 +9,8 @@ P = 128
 PACK = 4
 PASSES = K // (P * PACK)
 HALF = V // 2
+BLOCKS = S // P
+EARLY = 3
 FLOPS = 2 * K * V * N
 
 F32 = mybir.dt.float32
@@ -20,6 +22,8 @@ U8 = mybir.dt.uint8
 FP8X4 = mybir.dt.float8_e4m3fn_x4
 MULT = mybir.AluOpType.mult
 ADD = mybir.AluOpType.add
+MAX = mybir.AluOpType.max
+COPY = mybir.ActivationFunctionType.Copy
 RELU = mybir.ActivationFunctionType.Relu
 
 
@@ -38,30 +42,33 @@ def tile_picked_bag_lin_relu_sub_l_kernel(tc, xT, w_words, w_scales, b, gate, of
         warm = keep.tile([P, 1], F32, name="warm")
         warm_out = keep.tile([P, 1], F32, name="warm_out")
         weighted = [keep.tile([P, PACK, S], F32, name="weighted%d" % a) for a in range(PASSES)]
-        sums = [keep.tile([P, V, PACK], BF16, name="sums%d" % a, align_bytes=64) for a in range(PASSES)]
+        sums = [keep.tile([P, V, PACK], BF16, name="sums0", tag="sums", align_bytes=64)]
         x_codes = [keep.tile([P, V], U32, name="x_codes%d" % a, align_bytes=64) for a in range(PASSES)]
         x_plane = [keep.tile([P, V], U8, name="x_plane%d" % a, align_bytes=64) for a in range(PASSES)]
-        acc = [psum.tile([P, HALF], F32, name="acc%d" % h) for h in range(2)]
         result = [keep.tile([P, HALF], F32, name="result%d" % h) for h in range(2)]
 
         ident_f32 = keep.tile([P, P], F32, name="ident_f32")
-        ident_bf16 = keep.tile([P, P], BF16, name="ident_bf16")
-        turned = [psum.tile([P, PACK, P], F32, name="turned%d" % h) for h in range(2)]
-        rounded = [keep.tile([P, PACK, P], BF16, name="rounded%d" % h) for h in range(2)]
-        back = [psum.tile([P, PACK, P], BF16, name="back%d" % h) for h in range(2)]
+        gate_rows = keep.tile([P, P], F32, name="gate_rows")
+        gate_turned = psum.tile([P, P], F32, name="gate_turned", tag="shared")
+        gate_cols = keep.tile([P, BLOCKS], F32, name="gate_cols")
+        gate_spread = [psum.tile([P, V], F32, name="gate_spread%d" % d, tag="twice%d" % d) for d in range(D)]
+        turned = [psum.tile([P, BLOCKS, P], F32, name="turned%d" % j) for j in range(2)]
+        scaled = [keep.tile([P, BLOCKS, P], F32, name="scaled%d" % t) for t in range(EARLY)]
+        summed = [keep.tile([P, 2, P], F32, name="summed%d" % t) for t in range(PACK - EARLY)]
+        back = [psum.tile([P, PACK, P], F32, name="back%d" % h) for h in range(2)]
 
         x_rows = xT.rearrange("(a p t) c -> a t p c", a=PASSES, t=PACK)
 
-        nc.gpsimd.memset(w_plane[:].rearrange("p a m -> p (a m)").bitcast(U32), 0)
-        nc.gpsimd.memset(warm[:], 0.0)
+        nc.vector.memset(gate_rows[:], 0.0)
+        nc.vector.memset(warm[:], 0.0)
+        nc.vector.memset(w_plane[:].rearrange("p a m -> p (a m)").bitcast(U32), 0)
         make_identity(nc, ident_f32[:])
-        make_identity(nc, ident_bf16[:])
         nc.scalar.activation(warm_out[:], warm[:], RELU)
 
-        nc.sync.dma_start(offsets[:], offs)
-        nc.sync.dma_start(gates[:, 0:V], gate[0])
         nc.sync.dma_start(rows[0][:], x_rows[0, 0])
-        nc.sync.dma_start(gates[:, V:S], gate[1])
+        nc.sync.dma_start(offsets[:], offs)
+        gate_halves = gate.rearrange("d r (h v) -> (d r h) v", h=2)
+        nc.sync.dma_start(gate_rows[0:BLOCKS, :], gate_halves[0 : 3 * (P + 1) + 1 : P + 1, :])
         for i in range(1, PASSES * PACK):
             nc.sync.dma_start(rows[i][:], x_rows[i // PACK, i % PACK])
         nc.sync.dma_start(w_codes[:].bitcast(I32), w_words.rearrange("a p m r -> p a (m r)").bitcast(I32))
@@ -88,23 +95,50 @@ def tile_picked_bag_lin_relu_sub_l_kernel(tc, xT, w_words, w_scales, b, gate, of
                 ADD,
             )
 
-        def turn_and_sum(t):
+        def spread_gates():
+            nc.tensor.transpose(gate_turned[:], gate_rows[:], ident_f32[:])
+            nc.scalar.copy(gate_cols[:], gate_turned[:, 0:BLOCKS])
+            for d in range(D):
+                for h in range(2):
+                    column = gate_cols[:, 2 * d + h : 2 * d + h + 1]
+                    nc.tensor.transpose(gate_spread[d][:, h * P : (h + 1) * P], column.to_broadcast([P, P]), ident_f32[:])
+                nc.scalar.copy(gates[:, d * V : (d + 1) * V], gate_spread[d][:])
+
+        def pick(t):
+            nc.vector.tensor_copy(weighted[0][:, t, :], rows[t][:].indirect(offsets[:]))
+
+        def weigh_and_sum(t):
+            bank = turned[t % 2]
+            for j in range(BLOCKS):
+                nc.tensor.transpose(bank[:, j, :], weighted[0][:, t, j * P : (j + 1) * P], ident_f32[:])
+            for j in range(BLOCKS):
+                nc.scalar.activation(scaled[t][:, j, :], bank[:, j, :], COPY, scale=gate_cols[:, j : j + 1])
             for h in range(2):
                 for d in range(D):
-                    first = d * V + h * HALF
                     nc.tensor.matmul(
-                        turned[h][:, t, :],
-                        weighted[0][:, t, first : first + HALF],
+                        back[h][:, t, :],
+                        scaled[t][:, 2 * d + h, :],
                         ident_f32[:],
                         start=(d == 0),
                         stop=(d == D - 1),
                         is_transpose=True,
                     )
 
-        def turn_back(h):
-            nc.scalar.copy(rounded[h][:], turned[h][:])
-            for t in range(PACK):
-                nc.tensor.transpose(back[h][:, t, :], rounded[h][:, t, :], ident_bf16[:])
+        def turn_and_sum(t, bank):
+            for h in range(2):
+                for d in range(D):
+                    first = d * V + h * HALF
+                    nc.tensor.matmul(
+                        bank[:, t - EARLY, h, :],
+                        weighted[0][:, t, first : first + HALF],
+                        ident_f32[:],
+                        start=(d == 0),
+                        stop=(d == D - 1),
+                        is_transpose=True,
+                    )
+            nc.scalar.copy(summed[t - EARLY][:], bank[:, t - EARLY])
+            for h in range(2):
+                nc.tensor.transpose(back[h][:, t, :], summed[t - EARLY][:, h, :], ident_f32[:])
 
         def interleave(h):
             nc.scalar.copy(sums[0][:, h * HALF : (h + 1) * HALF, :], back[h][:].rearrange("p t v -> p v t"))
@@ -116,7 +150,7 @@ def tile_picked_bag_lin_relu_sub_l_kernel(tc, xT, w_words, w_scales, b, gate, of
                 in_=sums[a][:, first : first + count, :].rearrange("p v t -> p (v t)"),
             )
 
-        def multiply(a, h):
+        def multiply(acc, a, h):
             cols = slice(h * HALF, (h + 1) * HALF)
             nc.tensor.matmul_mx(
                 out=acc[h][:],
@@ -128,34 +162,32 @@ def tile_picked_bag_lin_relu_sub_l_kernel(tc, xT, w_words, w_scales, b, gate, of
                 stop=(a == PASSES - 1),
             )
 
-        def finish(h):
-            nc.scalar.activation(result[h][:], acc[h][:], RELU, bias=bias[:])
-            nc.sync.dma_start(out[:, h * HALF : (h + 1) * HALF], result[h][:])
-
-        gather(0, 0, V)
-        gather(0, V, V)
-        turn_and_sum(0)
-        for i in range(1, PACK):
-            gather(i, 0, S)
-            turn_and_sum(i)
-        for h in range(2):
-            turn_back(h)
+        spread_gates()
+        for t in range(EARLY):
+            pick(t)
+            weigh_and_sum(t)
+        late_bank = psum.tile([P, PACK - EARLY, 2, P], F32, name="late_bank", tag="shared")
+        for t in range(EARLY, PACK):
+            gather(t, 0, S)
+            turn_and_sum(t, late_bank)
         for h in range(2):
             interleave(h)
         for i in range(PACK, 2 * PACK - 1):
             gather(i, 0, S)
         quantize(0, 0, V)
-        multiply(0, 0)
-        multiply(0, 1)
-        gather(7, 0, HALF)
-        gather(7, V, HALF)
-        gather(7, HALF, HALF)
-        add(1, 0, HALF)
-        gather(7, V + HALF, HALF)
-        quantize(1, 0, HALF)
-        multiply(1, 0)
-        finish(0)
-        add(1, HALF, HALF)
-        quantize(1, HALF, HALF)
-        multiply(1, 1)
-        finish(1)
+        acc = [psum.tile([P, HALF], F32, name="acc%d" % h, tag="twice%d" % h) for h in range(2)]
+        sums.append(keep.tile([P, V, PACK], BF16, name="sums1", tag="sums", align_bytes=64))
+        multiply(acc, 0, 0)
+        multiply(acc, 0, 1)
+        for h in range(2):
+            for d in range(D):
+                gather(7, d * V + h * HALF, HALF)
+        for h in range(2):
+            add(1, h * HALF, HALF)
+        for h in range(2):
+            quantize(1, h * HALF, HALF)
+            multiply(acc, 1, h)
+        nc.scalar.activation(result[0][:], acc[0][:], RELU, bias=bias[:])
+        nc.scalar.dma_start(out[:, 0:HALF], result[0][:])
+        nc.vector.tensor_scalar(result[1][:], acc[1][:], bias[:], 0.0, ADD, MAX)
+        nc.sync.dma_start(out[:, HALF:V], result[1][:])

@@ -8,9 +8,10 @@ S = D * V
 P = 128
 PACK = 4
 PASSES = K // (P * PACK)
-HALF = V // 2
+HALVES = V // P
 BLOCKS = S // P
-EARLY = 3
+QUADRANTS = 4
+RUN = 2
 FLOPS = 2 * K * V * N
 
 F32 = mybir.dt.float32
@@ -34,160 +35,123 @@ def tile_picked_bag_lin_relu_sub_l_kernel(tc, xT, w_words, w_scales, b, gate, of
         psum = ctx.enter_context(tc.psum_pool(name="psum", bufs=1))
 
         offsets = keep.tile([P, S // 16], U16, name="offsets")
-        gates = keep.tile([P, S], F32, name="gates")
-        rows = [keep.tile([P, T], F32, name="rows%d" % i) for i in range(PASSES * PACK)]
+        planes = [[keep.tile([P, T], F32, name="plane%d%d" % (a, t)) for t in range(PACK)] for a in range(PASSES)]
         w_codes = keep.tile([P, PASSES, N * PACK], U8, name="w_codes", align_bytes=64)
-        w_plane = keep.tile([P, PASSES, N], U8, name="w_plane", align_bytes=64)
+        w_scale = keep.tile([P, PASSES, N], U8, name="w_scale", align_bytes=64)
         bias = keep.tile([P, 1], F32, name="bias")
-        warm = keep.tile([P, 1], F32, name="warm")
-        warm_out = keep.tile([P, 1], F32, name="warm_out")
-        weighted = [keep.tile([P, PACK, S], F32, name="weighted%d" % a) for a in range(PASSES)]
-        sums = [keep.tile([P, V, PACK], BF16, name="sums0", tag="sums", align_bytes=64)]
-        x_codes = [keep.tile([P, V], U32, name="x_codes%d" % a, align_bytes=64) for a in range(PASSES)]
-        x_plane = [keep.tile([P, V], U8, name="x_plane%d" % a, align_bytes=64) for a in range(PASSES)]
-        result = [keep.tile([P, HALF], F32, name="result%d" % h) for h in range(2)]
+        identity = keep.tile([P, P], F32, name="identity")
+        zero = keep.tile([P, 1], F32, name="zero")
+        relu_of_zero = keep.tile([P, 1], F32, name="relu_of_zero")
 
-        ident_f32 = keep.tile([P, P], F32, name="ident_f32")
         gate_rows = keep.tile([P, P], F32, name="gate_rows")
-        gate_turned = psum.tile([P, P], F32, name="gate_turned", tag="shared")
         gate_cols = keep.tile([P, BLOCKS], F32, name="gate_cols")
-        gate_spread = [psum.tile([P, V], F32, name="gate_spread%d" % d, tag="twice%d" % d) for d in range(D)]
-        turned = [psum.tile([P, BLOCKS, P], F32, name="turned%d" % j) for j in range(2)]
-        scaled = [keep.tile([P, BLOCKS, P], F32, name="scaled%d" % t) for t in range(EARLY)]
-        summed = [keep.tile([P, 2, P], F32, name="summed%d" % t) for t in range(PACK - EARLY)]
-        back = [psum.tile([P, PACK, P], F32, name="back%d" % h) for h in range(2)]
+        gates = keep.tile([P, S], F32, name="gates")
+        gate_cols_psum = psum.tile([P, P], F32, name="gate_cols_psum")
+        gates_psum = psum.tile([P, S], F32, name="gates_psum")
 
-        x_rows = xT.rearrange("(a p t) c -> a t p c", a=PASSES, t=PACK)
+        picked = keep.tile([P, PACK, S], F32, name="picked")
+        weighted = keep.tile([P, PACK, S], F32, name="weighted")
+        turned = [psum.tile([P, BLOCKS, P], F32, name="turned%d" % j) for j in range(2)]
+        scaled = [keep.tile([P, BLOCKS, P], F32, name="scaled%d" % t) for t in range(PACK)]
+        summed = [psum.tile([P, PACK, P], F32, name="summed%d" % h) for h in range(HALVES)]
+
+        x_codes = [keep.tile([P, V], U32, name="x_codes%d" % a, align_bytes=64) for a in range(PASSES)]
+        x_scale = [keep.tile([P, V], U8, name="x_scale%d" % a, align_bytes=64) for a in range(PASSES)]
+        acc = [psum.tile([P, P], F32, name="acc%d" % h) for h in range(HALVES)]
+        result = [keep.tile([P, P], F32, name="result%d" % h) for h in range(HALVES)]
+
+        def half(h):
+            return slice(h * P, (h + 1) * P)
 
         nc.vector.memset(gate_rows[:], 0.0)
-        nc.vector.memset(warm[:], 0.0)
-        nc.vector.memset(w_plane[:].rearrange("p a m -> p (a m)").bitcast(U32), 0)
-        make_identity(nc, ident_f32[:])
-        nc.scalar.activation(warm_out[:], warm[:], RELU)
+        nc.vector.memset(zero[:], 0.0)
+        nc.vector.memset(w_scale[:].rearrange("p a m -> p (a m)").bitcast(U32), 0)
+        make_identity(nc, identity[:])
+        nc.scalar.activation(relu_of_zero[:], zero[:], RELU)
 
-        nc.sync.dma_start(rows[0][:], x_rows[0, 0])
+        x_rows = xT.rearrange("(a p t) c -> a t p c", a=PASSES, t=PACK)
+        nc.sync.dma_start(planes[0][0][:], x_rows[0, 0])
         nc.sync.dma_start(offsets[:], offs)
-        gate_halves = gate.rearrange("d r (h v) -> (d r h) v", h=2)
-        nc.sync.dma_start(gate_rows[0:BLOCKS, :], gate_halves[0 : 3 * (P + 1) + 1 : P + 1, :])
+        gate_blocks = gate.rearrange("d r (h v) -> (d r h) v", h=HALVES)
+        nc.sync.dma_start(gate_rows[0:BLOCKS, :], gate_blocks[0 : (BLOCKS - 1) * (P + 1) + 1 : P + 1, :])
         for i in range(1, PASSES * PACK):
-            nc.sync.dma_start(rows[i][:], x_rows[i // PACK, i % PACK])
+            nc.sync.dma_start(planes[i // PACK][i % PACK][:], x_rows[i // PACK, i % PACK])
         nc.sync.dma_start(w_codes[:].bitcast(I32), w_words.rearrange("a p m r -> p a (m r)").bitcast(I32))
-        for q in range(4):
+        for q in range(QUADRANTS):
             nc.sync.dma_start(
-                w_plane[32 * q : 32 * q + 4, :, :].bitcast(I32),
+                w_scale[32 * q : 32 * q + 4, :, :].bitcast(I32),
                 w_scales[:, 4 * q : 4 * q + 4, :].rearrange("a q m -> q a m").bitcast(I32),
             )
         nc.sync.dma_start(bias[:], b)
 
-        def gather(i, first, count):
-            nc.vector.tensor_tensor(
-                weighted[i // PACK][:, i % PACK, first : first + count],
-                rows[i][:].indirect(offsets[:, first // 16 : (first + count) // 16]),
-                gates[:, first : first + count],
-                MULT,
-            )
-
-        def add(a, first, count):
-            nc.vector.tensor_tensor(
-                sums[a][:, first : first + count, :].rearrange("p (c i) t -> p c t i", i=2),
-                weighted[a][:, :, first : first + count].rearrange("p t (c i) -> p c t i", i=2),
-                weighted[a][:, :, V + first : V + first + count].rearrange("p t (c i) -> p c t i", i=2),
-                ADD,
-            )
-
-        def spread_gates():
-            nc.tensor.transpose(gate_turned[:], gate_rows[:], ident_f32[:])
-            nc.scalar.copy(gate_cols[:], gate_turned[:, 0:BLOCKS])
-            for d in range(D):
-                for h in range(2):
-                    column = gate_cols[:, 2 * d + h : 2 * d + h + 1]
-                    nc.tensor.transpose(gate_spread[d][:, h * P : (h + 1) * P], column.to_broadcast([P, P]), ident_f32[:])
-                nc.scalar.copy(gates[:, d * V : (d + 1) * V], gate_spread[d][:])
-
-        def pick(t):
-            nc.vector.tensor_copy(weighted[0][:, t, :], rows[t][:].indirect(offsets[:]))
-
-        def weigh_and_sum(t):
-            bank = turned[t % 2]
-            for j in range(BLOCKS):
-                nc.tensor.transpose(bank[:, j, :], weighted[0][:, t, j * P : (j + 1) * P], ident_f32[:])
-            for j in range(BLOCKS):
-                nc.scalar.activation(scaled[t][:, j, :], bank[:, j, :], COPY, scale=gate_cols[:, j : j + 1])
-            for h in range(2):
-                for d in range(D):
-                    nc.tensor.matmul(
-                        back[h][:, t, :],
-                        scaled[t][:, 2 * d + h, :],
-                        ident_f32[:],
-                        start=(d == 0),
-                        stop=(d == D - 1),
-                        is_transpose=True,
-                    )
-
-        def turn_and_sum(t, bank):
-            for h in range(2):
-                for d in range(D):
-                    first = d * V + h * HALF
-                    nc.tensor.matmul(
-                        bank[:, t - EARLY, h, :],
-                        weighted[0][:, t, first : first + HALF],
-                        ident_f32[:],
-                        start=(d == 0),
-                        stop=(d == D - 1),
-                        is_transpose=True,
-                    )
-            nc.scalar.copy(summed[t - EARLY][:], bank[:, t - EARLY])
-            for h in range(2):
-                nc.tensor.transpose(back[h][:, t, :], summed[t - EARLY][:, h, :], ident_f32[:])
-
-        def interleave(h):
-            nc.scalar.copy(sums[0][:, h * HALF : (h + 1) * HALF, :], back[h][:].rearrange("p t v -> p v t"))
-
-        def quantize(a, first, count):
+        def quantize(a, sums, bags):
             nc.vector.quantize_mx(
-                out=x_codes[a][:, first : first + count].bitcast(FP8X4),
-                scales=x_plane[a][:, first : first + count],
-                in_=sums[a][:, first : first + count, :].rearrange("p v t -> p (v t)"),
+                out=x_codes[a][:, bags].bitcast(FP8X4),
+                scales=x_scale[a][:, bags],
+                in_=sums[:, bags, :].rearrange("p v t -> p (v t)"),
             )
 
-        def multiply(acc, a, h):
-            cols = slice(h * HALF, (h + 1) * HALF)
+        def multiply(a, h):
             nc.tensor.matmul_mx(
                 out=acc[h][:],
                 lhsT=w_codes[:, a, :].bitcast(FP8X4),
-                lhsT_scale=w_plane[:, a, :],
-                rhs=x_codes[a][:, cols].bitcast(FP8X4),
-                rhs_scale=x_plane[a][:, cols],
+                lhsT_scale=w_scale[:, a, :],
+                rhs=x_codes[a][:, half(h)].bitcast(FP8X4),
+                rhs_scale=x_scale[a][:, half(h)],
                 start=(a == 0),
                 stop=(a == PASSES - 1),
             )
 
-        spread_gates()
-        for t in range(EARLY):
-            pick(t)
-            weigh_and_sum(t)
-        late_bank = psum.tile([P, PACK - EARLY, 2, P], F32, name="late_bank", tag="shared")
-        for t in range(EARLY, PACK):
-            gather(t, 0, S)
-            turn_and_sum(t, late_bank)
-        for h in range(2):
-            interleave(h)
-        for i in range(PACK, 2 * PACK - 1):
-            gather(i, 0, S)
-        quantize(0, 0, V)
-        acc = [psum.tile([P, HALF], F32, name="acc%d" % h, tag="twice%d" % h) for h in range(2)]
-        sums.append(keep.tile([P, V, PACK], BF16, name="sums1", tag="sums", align_bytes=64))
-        multiply(acc, 0, 0)
-        multiply(acc, 0, 1)
-        for h in range(2):
-            for d in range(D):
-                gather(7, d * V + h * HALF, HALF)
-        for h in range(2):
-            add(1, h * HALF, HALF)
-        for h in range(2):
-            quantize(1, h * HALF, HALF)
-            multiply(acc, 1, h)
+        nc.tensor.transpose(gate_cols_psum[:], gate_rows[:], identity[:])
+        nc.scalar.copy(gate_cols[:], gate_cols_psum[:, 0:BLOCKS])
+        for j in range(BLOCKS):
+            nc.tensor.transpose(gates_psum[:, half(j)], gate_cols[:, j : j + 1].to_broadcast([P, P]), identity[:])
+        nc.scalar.copy(gates[:], gates_psum[:])
+
+        for t in range(PACK):
+            nc.vector.tensor_copy(picked[:, t, :], planes[0][t][:].indirect(offsets[:]))
+            bank = turned[t % 2]
+            for j in range(BLOCKS):
+                nc.tensor.transpose(bank[:, j, :], picked[:, t, half(j)], identity[:])
+            for h in range(HALVES):
+                for j in range(h, BLOCKS, HALVES):
+                    nc.scalar.activation(scaled[t][:, j, :], bank[:, j, :], COPY, scale=gate_cols[:, j : j + 1])
+                for d in range(D):
+                    nc.tensor.matmul(
+                        summed[h][:, t, :],
+                        scaled[t][:, HALVES * d + h, :],
+                        identity[:],
+                        start=(d == 0),
+                        stop=(d == D - 1),
+                        is_transpose=True,
+                    )
+        sums0 = keep.tile([P, V, PACK], BF16, name="sums0", tag="sums", align_bytes=64)
+        for h in range(HALVES):
+            nc.scalar.copy(sums0[:, half(h), :], summed[h][:].rearrange("p t v -> p v t"))
+
+        def gather_weighted(t):
+            nc.vector.tensor_tensor(weighted[:, t, :], planes[1][t][:].indirect(offsets[:]), gates[:], MULT)
+
+        for t in range(PACK - 1):
+            gather_weighted(t)
+        quantize(0, sums0, slice(0, V))
+        for h in range(HALVES):
+            multiply(0, h)
+        gather_weighted(PACK - 1)
+
+        sums1 = keep.tile([P, V, PACK], BF16, name="sums1", tag="sums", align_bytes=64)
+        for h in range(HALVES):
+            nc.vector.tensor_tensor(
+                sums1[:, half(h), :].rearrange("p (c i) t -> p c t i", i=RUN),
+                weighted[:, :, half(h)].rearrange("p t (c i) -> p c t i", i=RUN),
+                weighted[:, :, half(HALVES + h)].rearrange("p t (c i) -> p c t i", i=RUN),
+                ADD,
+            )
+        for h in range(HALVES):
+            quantize(1, sums1, half(h))
+            multiply(1, h)
+
         nc.scalar.activation(result[0][:], acc[0][:], RELU, bias=bias[:])
-        nc.scalar.dma_start(out[:, 0:HALF], result[0][:])
+        nc.scalar.dma_start(out[:, half(0)], result[0][:])
         nc.vector.tensor_scalar(result[1][:], acc[1][:], bias[:], 0.0, ADD, MAX)
-        nc.sync.dma_start(out[:, HALF:V], result[1][:])
+        nc.sync.dma_start(out[:, half(1)], result[1][:])

@@ -11,6 +11,8 @@ PASSES = K // (P * PACK)
 HALVES = V // P
 BLOCKS = S // P
 QUADRANTS = 4
+LATE = 2
+TURNED = PASSES * PACK - LATE
 RUN = 2
 FLOPS = 2 * K * V * N
 
@@ -46,14 +48,13 @@ def tile_picked_bag_lin_relu_sub_l_kernel(tc, xT, w_words, w_scales, b, gate, of
         gate_rows = keep.tile([P, P], F32, name="gate_rows")
         gate_cols = keep.tile([P, BLOCKS], F32, name="gate_cols")
         gates = keep.tile([P, S], F32, name="gates")
-        gate_cols_psum = psum.tile([P, P], F32, name="gate_cols_psum")
-        gates_psum = psum.tile([P, S], F32, name="gates_psum")
+        gate_cols_psum = psum.tile([P, P], F32, name="gate_cols_psum", tag="spare0")
+        gates_psum = psum.tile([P, S], F32, name="gates_psum", tag="spare1")
 
-        picked = keep.tile([P, PACK, S], F32, name="picked")
-        weighted = keep.tile([P, PACK, S], F32, name="weighted")
+        picked = keep.tile([P, TURNED, S], F32, name="picked")
+        weighted = keep.tile([P, LATE, S], F32, name="weighted")
         turned = [psum.tile([P, BLOCKS, P], F32, name="turned%d" % j) for j in range(2)]
-        scaled = [keep.tile([P, BLOCKS, P], F32, name="scaled%d" % t) for t in range(PACK)]
-        summed = [psum.tile([P, PACK, P], F32, name="summed%d" % h) for h in range(HALVES)]
+        scaled = [keep.tile([P, BLOCKS, P], F32, name="scaled%d" % t) for t in range(TURNED)]
 
         x_codes = [keep.tile([P, V], U32, name="x_codes%d" % a, align_bytes=64) for a in range(PASSES)]
         x_scale = [keep.tile([P, V], U8, name="x_scale%d" % a, align_bytes=64) for a in range(PASSES)]
@@ -108,41 +109,48 @@ def tile_picked_bag_lin_relu_sub_l_kernel(tc, xT, w_words, w_scales, b, gate, of
             nc.tensor.transpose(gates_psum[:, half(j)], gate_cols[:, j : j + 1].to_broadcast([P, P]), identity[:])
         nc.scalar.copy(gates[:], gates_psum[:])
 
-        for t in range(PACK):
-            nc.vector.tensor_copy(picked[:, t, :], planes[0][t][:].indirect(offsets[:]))
-            bank = turned[t % 2]
+        def weigh_turned(i, summed):
+            a, t = divmod(i, PACK)
+            nc.vector.tensor_copy(picked[:, i, :], planes[a][t][:].indirect(offsets[:]))
+            bank = turned[i % 2]
             for j in range(BLOCKS):
-                nc.tensor.transpose(bank[:, j, :], picked[:, t, half(j)], identity[:])
+                nc.tensor.transpose(bank[:, j, :], picked[:, i, half(j)], identity[:])
             for h in range(HALVES):
                 for j in range(h, BLOCKS, HALVES):
-                    nc.scalar.activation(scaled[t][:, j, :], bank[:, j, :], COPY, scale=gate_cols[:, j : j + 1])
+                    nc.scalar.activation(scaled[i][:, j, :], bank[:, j, :], COPY, scale=gate_cols[:, j : j + 1])
                 for d in range(D):
                     nc.tensor.matmul(
                         summed[h][:, t, :],
-                        scaled[t][:, HALVES * d + h, :],
+                        scaled[i][:, HALVES * d + h, :],
                         identity[:],
                         start=(d == 0),
                         stop=(d == D - 1),
                         is_transpose=True,
                     )
-        sums0 = keep.tile([P, V, PACK], BF16, name="sums0", tag="sums", align_bytes=64)
+
+        summed0 = [psum.tile([P, PACK, P], F32, name="summed0%d" % h) for h in range(HALVES)]
+        for i in range(PACK):
+            weigh_turned(i, summed0)
+        sums0 = keep.tile([P, V, PACK], BF16, name="sums0", align_bytes=64)
         for h in range(HALVES):
-            nc.scalar.copy(sums0[:, half(h), :], summed[h][:].rearrange("p t v -> p v t"))
+            nc.scalar.copy(sums0[:, half(h), :], summed0[h][:].rearrange("p t v -> p v t"))
 
-        def gather_weighted(t):
-            nc.vector.tensor_tensor(weighted[:, t, :], planes[1][t][:].indirect(offsets[:]), gates[:], MULT)
+        summed1 = [psum.tile([P, PACK - LATE, P], F32, name="summed1%d" % h, tag="spare%d" % h) for h in range(HALVES)]
+        for i in range(PACK, TURNED):
+            weigh_turned(i, summed1)
+        sums1 = keep.tile([P, V, PACK], BF16, name="sums1", align_bytes=64)
+        for h in range(HALVES):
+            nc.scalar.copy(sums1[:, half(h), 0 : PACK - LATE], summed1[h][:].rearrange("p t v -> p v t"))
 
-        for t in range(PACK - 1):
-            gather_weighted(t)
+        for t in range(LATE):
+            nc.vector.tensor_tensor(weighted[:, t, :], planes[1][PACK - LATE + t][:].indirect(offsets[:]), gates[:], MULT)
         quantize(0, sums0, slice(0, V))
         for h in range(HALVES):
             multiply(0, h)
-        gather_weighted(PACK - 1)
 
-        sums1 = keep.tile([P, V, PACK], BF16, name="sums1", tag="sums", align_bytes=64)
         for h in range(HALVES):
             nc.vector.tensor_tensor(
-                sums1[:, half(h), :].rearrange("p (c i) t -> p c t i", i=RUN),
+                sums1[:, half(h), PACK - LATE : PACK].rearrange("p (c i) t -> p c t i", i=RUN),
                 weighted[:, :, half(h)].rearrange("p t (c i) -> p c t i", i=RUN),
                 weighted[:, :, half(HALVES + h)].rearrange("p t (c i) -> p c t i", i=RUN),
                 ADD,

@@ -11,8 +11,8 @@ PASSES = K // (P * PACK)
 HALVES = V // P
 BLOCKS = S // P
 QUADRANTS = 4
-LATE = 2
-TURNED = PASSES * PACK - LATE
+PAIR = 2
+PAIRS = PACK // PAIR
 RUN = 2
 FLOPS = 2 * K * V * N
 
@@ -45,21 +45,23 @@ def tile_picked_bag_lin_relu_sub_l_kernel(tc, xT, w_words, w_scales, b, gate, of
         zero = keep.tile([P, 1], F32, name="zero")
         relu_of_zero = keep.tile([P, 1], F32, name="relu_of_zero")
 
+        gate_runs = keep.tile([P, BLOCKS], F32, name="gate_runs")
         gate_rows = keep.tile([P, P], F32, name="gate_rows")
         gate_cols = keep.tile([P, BLOCKS], F32, name="gate_cols")
         gates = keep.tile([P, S], F32, name="gates")
-        gate_cols_psum = psum.tile([P, P], F32, name="gate_cols_psum", tag="spare0")
-        gates_psum = psum.tile([P, S], F32, name="gates_psum", tag="spare1")
+        gate_cols_psum = psum.tile([P, P], F32, name="gate_cols_psum", tag="words0")
+        gates_psum = psum.tile([P, BLOCKS, P], F32, name="gates_psum", tag="words1")
 
-        picked = keep.tile([P, TURNED, S], F32, name="picked")
-        weighted = keep.tile([P, LATE, S], F32, name="weighted")
-        turned = [psum.tile([P, BLOCKS, P], F32, name="turned%d" % j) for j in range(2)]
-        scaled = [keep.tile([P, BLOCKS, P], F32, name="scaled%d" % t) for t in range(TURNED)]
-
-        x_codes = [keep.tile([P, V], U32, name="x_codes%d" % a, align_bytes=64) for a in range(PASSES)]
-        x_scale = [keep.tile([P, V], U8, name="x_scale%d" % a, align_bytes=64) for a in range(PASSES)]
+        weighted = [keep.tile([P, PAIR, S], F32, name="weighted%d" % q) for q in range(PASSES * PAIRS)]
+        sums = [keep.tile([P, V, PACK], BF16, name="sums%d" % a, align_bytes=64) for a in range(PASSES)]
+        last_gates = keep.tile([P, V], F32, name="last_gates", tag="codes0", align_bytes=64)
+        x_scale1 = keep.tile([P, V], U8, name="x_scale1", align_bytes=64)
+        x_scale0 = keep.tile([P, V], U8, name="x_scale0", align_bytes=64)
+        x_scale = [x_scale0[:], x_scale1[:]]
         acc = [psum.tile([P, P], F32, name="acc%d" % h) for h in range(HALVES)]
         result = [keep.tile([P, P], F32, name="result%d" % h) for h in range(HALVES)]
+
+        x_codes = []
 
         def half(h):
             return slice(h * P, (h + 1) * P)
@@ -73,23 +75,25 @@ def tile_picked_bag_lin_relu_sub_l_kernel(tc, xT, w_words, w_scales, b, gate, of
         x_rows = xT.rearrange("(a p t) c -> a t p c", a=PASSES, t=PACK)
         nc.sync.dma_start(planes[0][0][:], x_rows[0, 0])
         nc.sync.dma_start(offsets[:], offs)
+        runs = gate.rearrange("d r (c i) -> (d r c) i", i=BLOCKS)
+        nc.sync.dma_start(gate_runs[:], runs[0 : (P - 1) * (P + 1) + 1 : P + 1, :])
         gate_blocks = gate.rearrange("d r (h v) -> (d r h) v", h=HALVES)
         nc.sync.dma_start(gate_rows[0:BLOCKS, :], gate_blocks[0 : (BLOCKS - 1) * (P + 1) + 1 : P + 1, :])
         for i in range(1, PASSES * PACK):
             nc.sync.dma_start(planes[i // PACK][i % PACK][:], x_rows[i // PACK, i % PACK])
-        nc.sync.dma_start(w_codes[:].bitcast(I32), w_words.rearrange("a p m r -> p a (m r)").bitcast(I32))
         for q in range(QUADRANTS):
             nc.sync.dma_start(
                 w_scale[32 * q : 32 * q + 4, :, :].bitcast(I32),
                 w_scales[:, 4 * q : 4 * q + 4, :].rearrange("a q m -> q a m").bitcast(I32),
             )
+        nc.sync.dma_start(w_codes[:].bitcast(I32), w_words.rearrange("a p m r -> p a (m r)").bitcast(I32))
         nc.sync.dma_start(bias[:], b)
 
-        def quantize(a, sums, bags):
+        def quantize(a, bags):
             nc.vector.quantize_mx(
                 out=x_codes[a][:, bags].bitcast(FP8X4),
                 scales=x_scale[a][:, bags],
-                in_=sums[:, bags, :].rearrange("p v t -> p (v t)"),
+                in_=sums[a][:, bags, :].rearrange("p v t -> p (v t)"),
             )
 
         def multiply(a, h):
@@ -103,60 +107,103 @@ def tile_picked_bag_lin_relu_sub_l_kernel(tc, xT, w_words, w_scales, b, gate, of
                 stop=(a == PASSES - 1),
             )
 
+        for i in range(BLOCKS):
+            nc.tensor.transpose(gates_psum[:, i, :], gate_runs[:, i : i + 1].to_broadcast([P, P]), identity[:])
+        nc.scalar.copy(gates[:].rearrange("m (p i) -> m p i", i=BLOCKS), gates_psum[:].rearrange("m i p -> m p i"))
+        nc.scalar.copy(last_gates[:], gates[:, 0:V])
         nc.tensor.transpose(gate_cols_psum[:], gate_rows[:], identity[:])
         nc.scalar.copy(gate_cols[:], gate_cols_psum[:, 0:BLOCKS])
-        for j in range(BLOCKS):
-            nc.tensor.transpose(gates_psum[:, half(j)], gate_cols[:, j : j + 1].to_broadcast([P, P]), identity[:])
-        nc.scalar.copy(gates[:], gates_psum[:])
 
-        def weigh_turned(i, summed):
-            a, t = divmod(i, PACK)
-            nc.vector.tensor_copy(picked[:, i, :], planes[a][t][:].indirect(offsets[:]))
-            bank = turned[i % 2]
-            for j in range(BLOCKS):
-                nc.tensor.transpose(bank[:, j, :], picked[:, i, half(j)], identity[:])
+        def gather_weighted(a, t):
+            nc.vector.tensor_tensor(
+                weighted[a * PAIRS + t // PAIR][:, t % PAIR, :], planes[a][t][:].indirect(offsets[:]), gates[:], MULT
+            )
+
+        def sum_turned(a, u, words):
+            q = a * PAIRS + u
+            turned = [psum.tile([P, PAIR, P], F32, name="turned%d%d" % (q, h), tag="turned%d%d" % (q % 2, h)) for h in range(HALVES)]
+            rounded = keep.tile([P, HALVES, P, PAIR], BF16, name="rounded%d" % q)
+            for e in range(PAIR):
+                gather_weighted(a, PAIR * u + e)
+                for h in range(HALVES):
+                    for d in range(D):
+                        nc.tensor.matmul(
+                            turned[h][:, e, :],
+                            weighted[q][:, e, half(HALVES * d + h)],
+                            identity[:],
+                            start=(d == 0),
+                            stop=(d == D - 1),
+                            is_transpose=True,
+                        )
             for h in range(HALVES):
-                for j in range(h, BLOCKS, HALVES):
-                    nc.scalar.activation(scaled[i][:, j, :], bank[:, j, :], COPY, scale=gate_cols[:, j : j + 1])
+                nc.scalar.copy(rounded[:, h, :, :], turned[h][:].rearrange("v e p -> v p e"))
+            for h in range(HALVES):
+                nc.tensor.transpose(
+                    words[h][:], rounded[:, h, :, :].rearrange("v p e -> v (p e)").bitcast(F32), identity[:]
+                )
+
+        def as_words(a):
+            return sums[a][:].rearrange("p v t -> p (v t)").bitcast(F32).rearrange("p (v u) -> p v u", u=PAIRS)
+
+        scaled = keep.tile([P, HALVES, D, PAIR, P], F32, name="scaled")
+        summed = [psum.tile([P, PAIR, P], F32, name="summed%d" % h, tag="words%d" % h) for h in range(HALVES)]
+        banks = [psum.tile([P, D, PAIR, P], F32, name="bank%d" % h, tag="turned0%d" % h) for h in range(HALVES)]
+        for e in range(PAIR):
+            nc.vector.tensor_copy(weighted[0][:, e, :], planes[0][e][:].indirect(offsets[:]))
+            for h in range(HALVES):
+                for d in range(D):
+                    nc.tensor.transpose(banks[h][:, d, e, :], weighted[0][:, e, half(HALVES * d + h)], identity[:])
+        for h in range(HALVES):
+            for d in range(D):
+                j = HALVES * d + h
+                nc.scalar.activation(scaled[:, h, d, :, :], banks[h][:, d, :, :], COPY, scale=gate_cols[:, j : j + 1])
+            for e in range(PAIR):
                 for d in range(D):
                     nc.tensor.matmul(
-                        summed[h][:, t, :],
-                        scaled[i][:, HALVES * d + h, :],
+                        summed[h][:, e, :],
+                        scaled[:, h, d, e, :],
                         identity[:],
                         start=(d == 0),
                         stop=(d == D - 1),
                         is_transpose=True,
                     )
-
-        summed0 = [psum.tile([P, PACK, P], F32, name="summed0%d" % h) for h in range(HALVES)]
-        for i in range(PACK):
-            weigh_turned(i, summed0)
-        sums0 = keep.tile([P, V, PACK], BF16, name="sums0", align_bytes=64)
         for h in range(HALVES):
-            nc.scalar.copy(sums0[:, half(h), :], summed0[h][:].rearrange("p t v -> p v t"))
+            nc.scalar.copy(sums[0][:, half(h), 0:PAIR], summed[h][:].rearrange("p e v -> p v e"))
 
-        summed1 = [psum.tile([P, PACK - LATE, P], F32, name="summed1%d" % h, tag="spare%d" % h) for h in range(HALVES)]
-        for i in range(PACK, TURNED):
-            weigh_turned(i, summed1)
-        sums1 = keep.tile([P, V, PACK], BF16, name="sums1", align_bytes=64)
-        for h in range(HALVES):
-            nc.scalar.copy(sums1[:, half(h), 0 : PACK - LATE], summed1[h][:].rearrange("p t v -> p v t"))
+        for a, u in ((0, 1), (1, 0)):
+            words = [psum.tile([P, P], F32, name="words%d%d" % (a, h), tag="words%d" % h) for h in range(HALVES)]
+            sum_turned(a, u, words)
+            for h in range(HALVES):
+                nc.scalar.copy(
+                    sums[a][:, half(h), PAIR * u : PAIR * (u + 1)],
+                    words[h][:].bitcast(BF16).rearrange("p (v e) -> p v e", e=PAIR),
+                )
 
-        for t in range(LATE):
-            nc.vector.tensor_tensor(weighted[:, t, :], planes[1][PACK - LATE + t][:].indirect(offsets[:]), gates[:], MULT)
-        quantize(0, sums0, slice(0, V))
-        for h in range(HALVES):
-            multiply(0, h)
+        gather_weighted(1, PACK - 2)
+        for first, end, factors in ((0, V, last_gates[:]), (V, V + P, gates[:, V : V + P]), (V + P, S, gates[:, V + P : S])):
+            nc.vector.tensor_tensor(
+                weighted[PASSES * PAIRS - 1][:, 1, first:end],
+                planes[1][PACK - 1][:].indirect(offsets[:, first // 16 : end // 16]),
+                factors,
+                MULT,
+            )
+        x_codes.append(keep.tile([P, V], U32, name="x_codes0", tag="codes0", align_bytes=64))
+        x_codes.append(keep.tile([P, V], U32, name="x_codes1", align_bytes=64))
 
+        last = weighted[PASSES * PAIRS - 1]
         for h in range(HALVES):
             nc.vector.tensor_tensor(
-                sums1[:, half(h), PACK - LATE : PACK].rearrange("p (c i) t -> p c t i", i=RUN),
-                weighted[:, :, half(h)].rearrange("p t (c i) -> p c t i", i=RUN),
-                weighted[:, :, half(HALVES + h)].rearrange("p t (c i) -> p c t i", i=RUN),
+                sums[1][:, half(h), PAIR:PACK].rearrange("p (c i) t -> p c t i", i=RUN),
+                last[:, :, half(h)].rearrange("p t (c i) -> p c t i", i=RUN),
+                last[:, :, half(HALVES + h)].rearrange("p t (c i) -> p c t i", i=RUN),
                 ADD,
             )
+            if h == 0:
+                quantize(0, slice(0, V))
         for h in range(HALVES):
-            quantize(1, sums1, half(h))
+            multiply(0, h)
+        for h in range(HALVES):
+            quantize(1, half(h))
             multiply(1, h)
 
         nc.scalar.activation(result[0][:], acc[0][:], RELU, bias=bias[:])

@@ -28,6 +28,7 @@ ADD = mybir.AluOpType.add
 MAX = mybir.AluOpType.max
 COPY = mybir.ActivationFunctionType.Copy
 RELU = mybir.ActivationFunctionType.Relu
+PICK = BF16
 
 
 def tile_picked_bag_lin_relu_sub_l_kernel(tc, xT, w_words, w_scales, b, gate, offs, out):
@@ -42,25 +43,23 @@ def tile_picked_bag_lin_relu_sub_l_kernel(tc, xT, w_words, w_scales, b, gate, of
         w_scale = keep.tile([P, PASSES, N], U8, name="w_scale", align_bytes=64)
         bias = keep.tile([P, 1], F32, name="bias")
         identity = keep.tile([P, P], F32, name="identity")
+        identity_bf16 = keep.tile([P, P], BF16, name="identity_bf16")
         zero = keep.tile([P, 1], F32, name="zero")
         relu_of_zero = keep.tile([P, 1], F32, name="relu_of_zero")
 
-        gate_runs = keep.tile([P, BLOCKS], F32, name="gate_runs")
         gate_rows = keep.tile([P, P], F32, name="gate_rows")
         gate_cols = keep.tile([P, BLOCKS], F32, name="gate_cols")
         gates = keep.tile([P, S], F32, name="gates")
-        gate_cols_psum = psum.tile([P, P], F32, name="gate_cols_psum", tag="words0")
-        gates_psum = psum.tile([P, BLOCKS, P], F32, name="gates_psum", tag="words1")
-
-        weighted = [keep.tile([P, PAIR, S], F32, name="weighted%d" % q) for q in range(PASSES * PAIRS)]
-        sums = [keep.tile([P, V, PACK], BF16, name="sums%d" % a, align_bytes=64) for a in range(PASSES)]
         last_gates = keep.tile([P, V], F32, name="last_gates", tag="codes0", align_bytes=64)
-        x_scale1 = keep.tile([P, V], U8, name="x_scale1", align_bytes=64)
-        x_scale0 = keep.tile([P, V], U8, name="x_scale0", align_bytes=64)
-        x_scale = [x_scale0[:], x_scale1[:]]
+        gate_cols_psum = psum.tile([P, P], F32, name="gate_cols_psum", tag="odd0")
+        gates_psum = psum.tile([P, S], F32, name="gates_psum", tag="odd1")
+
+        picked = [keep.tile([P, S], PICK, name="picked%d" % t) for t in range(PACK)]
+        weighted = [keep.tile([P, PAIR, S], F32, name="weighted%d" % u) for u in range(PAIRS)]
+        sums = [keep.tile([P, V, PACK], BF16, name="sums%d" % a, align_bytes=64) for a in range(PASSES)]
+        x_scale = [keep.tile([P, V], U8, name="x_scale%d" % a, align_bytes=64) for a in range(PASSES)]
         acc = [psum.tile([P, P], F32, name="acc%d" % h) for h in range(HALVES)]
         result = [keep.tile([P, P], F32, name="result%d" % h) for h in range(HALVES)]
-
         x_codes = []
 
         def half(h):
@@ -70,23 +69,22 @@ def tile_picked_bag_lin_relu_sub_l_kernel(tc, xT, w_words, w_scales, b, gate, of
         nc.vector.memset(zero[:], 0.0)
         nc.vector.memset(w_scale[:].rearrange("p a m -> p (a m)").bitcast(U32), 0)
         make_identity(nc, identity[:])
+        make_identity(nc, identity_bf16[:])
         nc.scalar.activation(relu_of_zero[:], zero[:], RELU)
 
         x_rows = xT.rearrange("(a p t) c -> a t p c", a=PASSES, t=PACK)
         nc.sync.dma_start(planes[0][0][:], x_rows[0, 0])
         nc.sync.dma_start(offsets[:], offs)
-        runs = gate.rearrange("d r (c i) -> (d r c) i", i=BLOCKS)
-        nc.sync.dma_start(gate_runs[:], runs[0 : (P - 1) * (P + 1) + 1 : P + 1, :])
         gate_blocks = gate.rearrange("d r (h v) -> (d r h) v", h=HALVES)
         nc.sync.dma_start(gate_rows[0:BLOCKS, :], gate_blocks[0 : (BLOCKS - 1) * (P + 1) + 1 : P + 1, :])
         for i in range(1, PASSES * PACK):
             nc.sync.dma_start(planes[i // PACK][i % PACK][:], x_rows[i // PACK, i % PACK])
+        nc.sync.dma_start(w_codes[:].bitcast(I32), w_words.rearrange("a p m r -> p a (m r)").bitcast(I32))
         for q in range(QUADRANTS):
             nc.sync.dma_start(
                 w_scale[32 * q : 32 * q + 4, :, :].bitcast(I32),
                 w_scales[:, 4 * q : 4 * q + 4, :].rearrange("a q m -> q a m").bitcast(I32),
             )
-        nc.sync.dma_start(w_codes[:].bitcast(I32), w_words.rearrange("a p m r -> p a (m r)").bitcast(I32))
         nc.sync.dma_start(bias[:], b)
 
         def quantize(a, bags):
@@ -107,82 +105,60 @@ def tile_picked_bag_lin_relu_sub_l_kernel(tc, xT, w_words, w_scales, b, gate, of
                 stop=(a == PASSES - 1),
             )
 
-        for i in range(BLOCKS):
-            nc.tensor.transpose(gates_psum[:, i, :], gate_runs[:, i : i + 1].to_broadcast([P, P]), identity[:])
-        nc.scalar.copy(gates[:].rearrange("m (p i) -> m p i", i=BLOCKS), gates_psum[:].rearrange("m i p -> m p i"))
-        nc.scalar.copy(last_gates[:], gates[:, 0:V])
+        def add_turned(total, parts):
+            for d in range(D):
+                nc.tensor.matmul(total, parts[d], identity[:], start=(d == 0), stop=(d == D - 1), is_transpose=True)
+
         nc.tensor.transpose(gate_cols_psum[:], gate_rows[:], identity[:])
         nc.scalar.copy(gate_cols[:], gate_cols_psum[:, 0:BLOCKS])
+        for j in range(BLOCKS):
+            nc.tensor.transpose(gates_psum[:, half(j)], gate_cols[:, j : j + 1].to_broadcast([P, P]), identity[:])
+        nc.scalar.copy(gates[:], gates_psum[:])
+        nc.scalar.copy(last_gates[:], gates_psum[:, 0:V])
 
-        def gather_weighted(a, t):
-            nc.vector.tensor_tensor(
-                weighted[a * PAIRS + t // PAIR][:, t % PAIR, :], planes[a][t][:].indirect(offsets[:]), gates[:], MULT
-            )
-
-        def sum_turned(a, u, words):
-            q = a * PAIRS + u
-            turned = [psum.tile([P, PAIR, P], F32, name="turned%d%d" % (q, h), tag="turned%d%d" % (q % 2, h)) for h in range(HALVES)]
-            rounded = keep.tile([P, HALVES, P, PAIR], BF16, name="rounded%d" % q)
+        summed = [psum.tile([P, PACK, P], F32, name="summed%d" % h) for h in range(HALVES)]
+        for u in range(PAIRS):
+            scaled = keep.tile([P, HALVES, D, PAIR, P], F32, name="scaled%d" % u)
+            banks = [
+                psum.tile([P, D, PAIR, P], PICK, name="bank%d%d" % (u, h), tag=("even%d", "odd%d")[u] % h)
+                for h in range(HALVES)
+            ]
             for e in range(PAIR):
-                gather_weighted(a, PAIR * u + e)
+                t = PAIR * u + e
+                nc.vector.tensor_copy(picked[t][:], planes[0][t][:].indirect(offsets[:]))
                 for h in range(HALVES):
                     for d in range(D):
-                        nc.tensor.matmul(
-                            turned[h][:, e, :],
-                            weighted[q][:, e, half(HALVES * d + h)],
-                            identity[:],
-                            start=(d == 0),
-                            stop=(d == D - 1),
-                            is_transpose=True,
-                        )
+                        nc.tensor.transpose(banks[h][:, d, e, :], picked[t][:, half(HALVES * d + h)], identity_bf16[:])
             for h in range(HALVES):
-                nc.scalar.copy(rounded[:, h, :, :], turned[h][:].rearrange("v e p -> v p e"))
-            for h in range(HALVES):
-                nc.tensor.transpose(
-                    words[h][:], rounded[:, h, :, :].rearrange("v p e -> v (p e)").bitcast(F32), identity[:]
-                )
+                for d in range(D):
+                    j = HALVES * d + h
+                    nc.scalar.activation(scaled[:, h, d, :, :], banks[h][:, d, :, :], COPY, scale=gate_cols[:, j : j + 1])
+                for e in range(PAIR):
+                    add_turned(summed[h][:, PAIR * u + e, :], [scaled[:, h, d, e, :] for d in range(D)])
+        for h in range(HALVES):
+            nc.scalar.copy(sums[0][:, half(h), :], summed[h][:].rearrange("p t v -> p v t"))
 
-        def as_words(a):
-            return sums[a][:].rearrange("p v t -> p (v t)").bitcast(F32).rearrange("p (v u) -> p v u", u=PAIRS)
-
-        scaled = keep.tile([P, HALVES, D, PAIR, P], F32, name="scaled")
-        summed = [psum.tile([P, PAIR, P], F32, name="summed%d" % h, tag="words%d" % h) for h in range(HALVES)]
-        banks = [psum.tile([P, D, PAIR, P], F32, name="bank%d" % h, tag="turned0%d" % h) for h in range(HALVES)]
+        turned = [psum.tile([P, PAIR, P], F32, name="turned%d" % h, tag="even%d" % h) for h in range(HALVES)]
+        rounded = [keep.tile([P, P, PAIR], BF16, name="rounded%d" % h) for h in range(HALVES)]
+        words = [psum.tile([P, P], F32, name="words%d" % h, tag="odd%d" % h) for h in range(HALVES)]
         for e in range(PAIR):
-            nc.vector.tensor_copy(weighted[0][:, e, :], planes[0][e][:].indirect(offsets[:]))
+            nc.vector.tensor_tensor(weighted[0][:, e, :], planes[1][e][:].indirect(offsets[:]), gates[:], MULT)
             for h in range(HALVES):
-                for d in range(D):
-                    nc.tensor.transpose(banks[h][:, d, e, :], weighted[0][:, e, half(HALVES * d + h)], identity[:])
+                add_turned(turned[h][:, e, :], [weighted[0][:, e, half(HALVES * d + h)] for d in range(D)])
         for h in range(HALVES):
-            for d in range(D):
-                j = HALVES * d + h
-                nc.scalar.activation(scaled[:, h, d, :, :], banks[h][:, d, :, :], COPY, scale=gate_cols[:, j : j + 1])
-            for e in range(PAIR):
-                for d in range(D):
-                    nc.tensor.matmul(
-                        summed[h][:, e, :],
-                        scaled[:, h, d, e, :],
-                        identity[:],
-                        start=(d == 0),
-                        stop=(d == D - 1),
-                        is_transpose=True,
-                    )
+            nc.scalar.copy(rounded[h][:], turned[h][:].rearrange("v e p -> v p e"))
         for h in range(HALVES):
-            nc.scalar.copy(sums[0][:, half(h), 0:PAIR], summed[h][:].rearrange("p e v -> p v e"))
+            nc.tensor.transpose(words[h][:], rounded[h][:].rearrange("v p e -> v (p e)").bitcast(F32), identity[:])
+        for h in range(HALVES):
+            nc.scalar.copy(
+                sums[1][:, half(h), 0:PAIR], words[h][:].bitcast(BF16).rearrange("p (v e) -> p v e", e=PAIR)
+            )
 
-        for a, u in ((0, 1), (1, 0)):
-            words = [psum.tile([P, P], F32, name="words%d%d" % (a, h), tag="words%d" % h) for h in range(HALVES)]
-            sum_turned(a, u, words)
-            for h in range(HALVES):
-                nc.scalar.copy(
-                    sums[a][:, half(h), PAIR * u : PAIR * (u + 1)],
-                    words[h][:].bitcast(BF16).rearrange("p (v e) -> p v e", e=PAIR),
-                )
-
-        gather_weighted(1, PACK - 2)
+        last = weighted[1]
+        nc.vector.tensor_tensor(last[:, 0, :], planes[1][PAIR][:].indirect(offsets[:]), gates[:], MULT)
         for first, end, factors in ((0, V, last_gates[:]), (V, V + P, gates[:, V : V + P]), (V + P, S, gates[:, V + P : S])):
             nc.vector.tensor_tensor(
-                weighted[PASSES * PAIRS - 1][:, 1, first:end],
+                last[:, 1, first:end],
                 planes[1][PACK - 1][:].indirect(offsets[:, first // 16 : end // 16]),
                 factors,
                 MULT,
@@ -190,7 +166,6 @@ def tile_picked_bag_lin_relu_sub_l_kernel(tc, xT, w_words, w_scales, b, gate, of
         x_codes.append(keep.tile([P, V], U32, name="x_codes0", tag="codes0", align_bytes=64))
         x_codes.append(keep.tile([P, V], U32, name="x_codes1", align_bytes=64))
 
-        last = weighted[PASSES * PAIRS - 1]
         for h in range(HALVES):
             nc.vector.tensor_tensor(
                 sums[1][:, half(h), PAIR:PACK].rearrange("p (c i) t -> p c t i", i=RUN),

@@ -13,6 +13,8 @@ BLOCKS = S // P
 QUADRANTS = 4
 PAIR = 2
 PAIRS = PACK // PAIR
+GROUP = 16
+CUT = S - P
 RUN = 2
 FLOPS = 2 * K * V * N
 
@@ -28,7 +30,6 @@ ADD = mybir.AluOpType.add
 MAX = mybir.AluOpType.max
 COPY = mybir.ActivationFunctionType.Copy
 RELU = mybir.ActivationFunctionType.Relu
-PICK = BF16
 
 
 def tile_picked_bag_lin_relu_sub_l_kernel(tc, xT, w_words, w_scales, b, gate, offs, out):
@@ -37,7 +38,7 @@ def tile_picked_bag_lin_relu_sub_l_kernel(tc, xT, w_words, w_scales, b, gate, of
         keep = ctx.enter_context(tc.tile_pool(name="keep", bufs=1))
         psum = ctx.enter_context(tc.psum_pool(name="psum", bufs=1))
 
-        offsets = keep.tile([P, S // 16], U16, name="offsets")
+        offsets = keep.tile([P, S // GROUP], U16, name="offsets")
         planes = [[keep.tile([P, T], F32, name="plane%d%d" % (a, t)) for t in range(PACK)] for a in range(PASSES)]
         w_codes = keep.tile([P, PASSES, N * PACK], U8, name="w_codes", align_bytes=64)
         w_scale = keep.tile([P, PASSES, N], U8, name="w_scale", align_bytes=64)
@@ -50,20 +51,22 @@ def tile_picked_bag_lin_relu_sub_l_kernel(tc, xT, w_words, w_scales, b, gate, of
         gate_rows = keep.tile([P, P], F32, name="gate_rows")
         gate_cols = keep.tile([P, BLOCKS], F32, name="gate_cols")
         gates = keep.tile([P, S], F32, name="gates")
-        last_gates = keep.tile([P, V], F32, name="last_gates", tag="codes0", align_bytes=64)
+        last_gates = keep.tile([P, CUT], F32, name="last_gates", tag="codes0", align_bytes=64)
         gate_cols_psum = psum.tile([P, P], F32, name="gate_cols_psum", tag="odd0")
         gates_psum = psum.tile([P, S], F32, name="gates_psum", tag="odd1")
 
-        picked = [keep.tile([P, S], PICK, name="picked%d" % t) for t in range(PACK)]
+        picked = [keep.tile([P, S], BF16, name="picked%d" % t) for t in range(PACK)]
         weighted = [keep.tile([P, PAIR, S], F32, name="weighted%d" % u) for u in range(PAIRS)]
         sums = [keep.tile([P, V, PACK], BF16, name="sums%d" % a, align_bytes=64) for a in range(PASSES)]
         x_scale = [keep.tile([P, V], U8, name="x_scale%d" % a, align_bytes=64) for a in range(PASSES)]
         acc = [psum.tile([P, P], F32, name="acc%d" % h) for h in range(HALVES)]
         result = [keep.tile([P, P], F32, name="result%d" % h) for h in range(HALVES)]
-        x_codes = []
 
         def half(h):
             return slice(h * P, (h + 1) * P)
+
+        def block(d, h):
+            return half(HALVES * d + h)
 
         nc.vector.memset(gate_rows[:], 0.0)
         nc.vector.memset(zero[:], 0.0)
@@ -87,6 +90,80 @@ def tile_picked_bag_lin_relu_sub_l_kernel(tc, xT, w_words, w_scales, b, gate, of
             )
         nc.sync.dma_start(bias[:], b)
 
+        def add_turned(total, parts):
+            for d in range(D):
+                nc.tensor.matmul(total, parts[d], identity[:], start=(d == 0), stop=(d == D - 1), is_transpose=True)
+
+        nc.tensor.transpose(gate_cols_psum[:], gate_rows[:], identity[:])
+        nc.scalar.copy(gate_cols[:], gate_cols_psum[:, 0:BLOCKS])
+        for j in range(BLOCKS):
+            nc.tensor.transpose(gates_psum[:, half(j)], gate_cols[:, j : j + 1].to_broadcast([P, P]), identity[:])
+        nc.scalar.copy(gates[:], gates_psum[:])
+        nc.scalar.copy(last_gates[:], gates_psum[:, 0:CUT])
+
+        summed = [psum.tile([P, PACK, P], F32, name="summed%d" % h) for h in range(HALVES)]
+        for u in range(PAIRS):
+            scaled = keep.tile([P, HALVES, D, PAIR, P], F32, name="scaled%d" % u)
+            entries = [
+                psum.tile([P, D, PAIR, P], BF16, name="entries%d%d" % (u, h), tag=("even%d", "odd%d")[u] % h)
+                for h in range(HALVES)
+            ]
+            for e in range(PAIR):
+                t = PAIR * u + e
+                nc.vector.tensor_copy(picked[t][:], planes[0][t][:].indirect(offsets[:]))
+                for h in range(HALVES):
+                    for d in range(D):
+                        nc.tensor.transpose(entries[h][:, d, e, :], picked[t][:, block(d, h)], identity_bf16[:])
+            for h in range(HALVES):
+                for d in range(D):
+                    j = HALVES * d + h
+                    nc.scalar.activation(
+                        scaled[:, h, d, :, :], entries[h][:, d, :, :], COPY, scale=gate_cols[:, j : j + 1]
+                    )
+                for e in range(PAIR):
+                    add_turned(summed[h][:, PAIR * u + e, :], [scaled[:, h, d, e, :] for d in range(D)])
+        for h in range(HALVES):
+            nc.scalar.copy(sums[0][:, half(h), :], summed[h][:].rearrange("p t v -> p v t"))
+
+        turned = [psum.tile([P, PAIR, P], F32, name="turned%d" % h, tag="even%d" % h) for h in range(HALVES)]
+        rounded = [keep.tile([P, P, PAIR], BF16, name="rounded%d" % h) for h in range(HALVES)]
+        words = [psum.tile([P, P], F32, name="words%d" % h, tag="odd%d" % h) for h in range(HALVES)]
+        for e in range(PAIR):
+            nc.vector.tensor_tensor(weighted[0][:, e, :], planes[1][e][:].indirect(offsets[:]), gates[:], MULT)
+            for h in range(HALVES):
+                add_turned(turned[h][:, e, :], [weighted[0][:, e, block(d, h)] for d in range(D)])
+        for h in range(HALVES):
+            nc.scalar.copy(rounded[h][:], turned[h][:].rearrange("v e p -> v p e"))
+        for h in range(HALVES):
+            nc.tensor.transpose(words[h][:], rounded[h][:].rearrange("v p e -> v (p e)").bitcast(F32), identity[:])
+        for h in range(HALVES):
+            nc.scalar.copy(
+                sums[1][:, half(h), 0:PAIR], words[h][:].bitcast(BF16).rearrange("p (v e) -> p v e", e=PAIR)
+            )
+
+        nc.vector.tensor_tensor(weighted[1][:, 0, :], planes[1][PAIR][:].indirect(offsets[:]), gates[:], MULT)
+        parts = ((0, CUT, last_gates[:]), (CUT, S, gates[:, CUT:S]))
+        for first, end, factors in parts:
+            nc.vector.tensor_tensor(
+                weighted[1][:, 1, first:end],
+                planes[1][PACK - 1][:].indirect(offsets[:, first // GROUP : end // GROUP]),
+                factors,
+                MULT,
+            )
+
+        x_codes = [
+            keep.tile([P, V], U32, name="x_codes0", tag="codes0", align_bytes=64),
+            keep.tile([P, V], U32, name="x_codes1", align_bytes=64),
+        ]
+
+        def add_pieces(h):
+            nc.vector.tensor_tensor(
+                sums[1][:, half(h), PAIR:PACK].rearrange("p (c i) t -> p c t i", i=RUN),
+                weighted[1][:, :, block(0, h)].rearrange("p t (c i) -> p c t i", i=RUN),
+                weighted[1][:, :, block(1, h)].rearrange("p t (c i) -> p c t i", i=RUN),
+                ADD,
+            )
+
         def quantize(a, bags):
             nc.vector.quantize_mx(
                 out=x_codes[a][:, bags].bitcast(FP8X4),
@@ -105,83 +182,16 @@ def tile_picked_bag_lin_relu_sub_l_kernel(tc, xT, w_words, w_scales, b, gate, of
                 stop=(a == PASSES - 1),
             )
 
-        def add_turned(total, parts):
-            for d in range(D):
-                nc.tensor.matmul(total, parts[d], identity[:], start=(d == 0), stop=(d == D - 1), is_transpose=True)
-
-        nc.tensor.transpose(gate_cols_psum[:], gate_rows[:], identity[:])
-        nc.scalar.copy(gate_cols[:], gate_cols_psum[:, 0:BLOCKS])
-        for j in range(BLOCKS):
-            nc.tensor.transpose(gates_psum[:, half(j)], gate_cols[:, j : j + 1].to_broadcast([P, P]), identity[:])
-        nc.scalar.copy(gates[:], gates_psum[:])
-        nc.scalar.copy(last_gates[:], gates_psum[:, 0:V])
-
-        summed = [psum.tile([P, PACK, P], F32, name="summed%d" % h) for h in range(HALVES)]
-        for u in range(PAIRS):
-            scaled = keep.tile([P, HALVES, D, PAIR, P], F32, name="scaled%d" % u)
-            banks = [
-                psum.tile([P, D, PAIR, P], PICK, name="bank%d%d" % (u, h), tag=("even%d", "odd%d")[u] % h)
-                for h in range(HALVES)
-            ]
-            for e in range(PAIR):
-                t = PAIR * u + e
-                nc.vector.tensor_copy(picked[t][:], planes[0][t][:].indirect(offsets[:]))
-                for h in range(HALVES):
-                    for d in range(D):
-                        nc.tensor.transpose(banks[h][:, d, e, :], picked[t][:, half(HALVES * d + h)], identity_bf16[:])
-            for h in range(HALVES):
-                for d in range(D):
-                    j = HALVES * d + h
-                    nc.scalar.activation(scaled[:, h, d, :, :], banks[h][:, d, :, :], COPY, scale=gate_cols[:, j : j + 1])
-                for e in range(PAIR):
-                    add_turned(summed[h][:, PAIR * u + e, :], [scaled[:, h, d, e, :] for d in range(D)])
-        for h in range(HALVES):
-            nc.scalar.copy(sums[0][:, half(h), :], summed[h][:].rearrange("p t v -> p v t"))
-
-        turned = [psum.tile([P, PAIR, P], F32, name="turned%d" % h, tag="even%d" % h) for h in range(HALVES)]
-        rounded = [keep.tile([P, P, PAIR], BF16, name="rounded%d" % h) for h in range(HALVES)]
-        words = [psum.tile([P, P], F32, name="words%d" % h, tag="odd%d" % h) for h in range(HALVES)]
-        for e in range(PAIR):
-            nc.vector.tensor_tensor(weighted[0][:, e, :], planes[1][e][:].indirect(offsets[:]), gates[:], MULT)
-            for h in range(HALVES):
-                add_turned(turned[h][:, e, :], [weighted[0][:, e, half(HALVES * d + h)] for d in range(D)])
-        for h in range(HALVES):
-            nc.scalar.copy(rounded[h][:], turned[h][:].rearrange("v e p -> v p e"))
-        for h in range(HALVES):
-            nc.tensor.transpose(words[h][:], rounded[h][:].rearrange("v p e -> v (p e)").bitcast(F32), identity[:])
-        for h in range(HALVES):
-            nc.scalar.copy(
-                sums[1][:, half(h), 0:PAIR], words[h][:].bitcast(BF16).rearrange("p (v e) -> p v e", e=PAIR)
-            )
-
-        last = weighted[1]
-        nc.vector.tensor_tensor(last[:, 0, :], planes[1][PAIR][:].indirect(offsets[:]), gates[:], MULT)
-        for first, end, factors in ((0, V, last_gates[:]), (V, V + P, gates[:, V : V + P]), (V + P, S, gates[:, V + P : S])):
-            nc.vector.tensor_tensor(
-                last[:, 1, first:end],
-                planes[1][PACK - 1][:].indirect(offsets[:, first // 16 : end // 16]),
-                factors,
-                MULT,
-            )
-        x_codes.append(keep.tile([P, V], U32, name="x_codes0", tag="codes0", align_bytes=64))
-        x_codes.append(keep.tile([P, V], U32, name="x_codes1", align_bytes=64))
-
-        for h in range(HALVES):
-            nc.vector.tensor_tensor(
-                sums[1][:, half(h), PAIR:PACK].rearrange("p (c i) t -> p c t i", i=RUN),
-                last[:, :, half(h)].rearrange("p t (c i) -> p c t i", i=RUN),
-                last[:, :, half(HALVES + h)].rearrange("p t (c i) -> p c t i", i=RUN),
-                ADD,
-            )
-            if h == 0:
-                quantize(0, slice(0, V))
+        add_pieces(0)
+        quantize(0, slice(0, V))
+        add_pieces(1)
         for h in range(HALVES):
             multiply(0, h)
         for h in range(HALVES):
             quantize(1, half(h))
             multiply(1, h)
 
-        nc.scalar.activation(result[0][:], acc[0][:], RELU, bias=bias[:])
-        nc.scalar.dma_start(out[:, half(0)], result[0][:])
-        nc.vector.tensor_scalar(result[1][:], acc[1][:], bias[:], 0.0, ADD, MAX)
-        nc.sync.dma_start(out[:, half(1)], result[1][:])
+        nc.vector.tensor_scalar(result[0][:], acc[0][:], bias[:], 0.0, ADD, MAX)
+        nc.sync.dma_start(out[:, half(0)], result[0][:])
+        nc.scalar.activation(result[1][:], acc[1][:], RELU, bias=bias[:])
+        nc.scalar.dma_start(out[:, half(1)], result[1][:])

@@ -51,15 +51,14 @@ def tile_picked_bag_lin_relu_sub_l_kernel(tc, xT, w_words, w_scales, b, gate, of
         gate_rows = keep.tile([P, P], F32, name="gate_rows")
         gate_cols = keep.tile([P, BLOCKS], F32, name="gate_cols")
         gates = keep.tile([P, S], F32, name="gates")
-        last_gates = keep.tile([P, CUT], F32, name="last_gates", tag="codes0", align_bytes=64)
         gate_cols_psum = psum.tile([P, P], F32, name="gate_cols_psum", tag="odd0")
         gates_psum = psum.tile([P, S], F32, name="gates_psum", tag="odd1")
 
         picked = [keep.tile([P, S], BF16, name="picked%d" % t) for t in range(PACK)]
-        weighted = [keep.tile([P, PAIR, S], F32, name="weighted%d" % u) for u in range(PAIRS)]
+        picked_first = keep.tile([P, S], BF16, name="picked_first")
+        weighted = keep.tile([P, PACK - 1, S], F32, name="weighted")
         sums = [keep.tile([P, V, PACK], BF16, name="sums%d" % a, align_bytes=64) for a in range(PASSES)]
         x_scale = [keep.tile([P, V], U8, name="x_scale%d" % a, align_bytes=64) for a in range(PASSES)]
-        acc = [psum.tile([P, P], F32, name="acc%d" % h) for h in range(HALVES)]
         result = [keep.tile([P, P], F32, name="result%d" % h) for h in range(HALVES)]
 
         def half(h):
@@ -76,12 +75,12 @@ def tile_picked_bag_lin_relu_sub_l_kernel(tc, xT, w_words, w_scales, b, gate, of
         nc.scalar.activation(relu_of_zero[:], zero[:], RELU)
 
         x_rows = xT.rearrange("(a p t) c -> a t p c", a=PASSES, t=PACK)
-        nc.sync.dma_start(planes[0][0][:], x_rows[0, 0])
+        nc.sync.dma_start(planes[1][0][:], x_rows[1, 0])
         nc.sync.dma_start(offsets[:], offs)
         gate_blocks = gate.rearrange("d r (h v) -> (d r h) v", h=HALVES)
         nc.sync.dma_start(gate_rows[0:BLOCKS, :], gate_blocks[0 : (BLOCKS - 1) * (P + 1) + 1 : P + 1, :])
-        for i in range(1, PASSES * PACK):
-            nc.sync.dma_start(planes[i // PACK][i % PACK][:], x_rows[i // PACK, i % PACK])
+        for a, t in [(0, t) for t in range(PACK)] + [(1, t) for t in range(1, PACK)]:
+            nc.sync.dma_start(planes[a][t][:], x_rows[a, t])
         nc.sync.dma_start(w_codes[:].bitcast(I32), w_words.rearrange("a p m r -> p a (m r)").bitcast(I32))
         for q in range(QUADRANTS):
             nc.sync.dma_start(
@@ -99,6 +98,22 @@ def tile_picked_bag_lin_relu_sub_l_kernel(tc, xT, w_words, w_scales, b, gate, of
         for j in range(BLOCKS):
             nc.tensor.transpose(gates_psum[:, half(j)], gate_cols[:, j : j + 1].to_broadcast([P, P]), identity[:])
         nc.scalar.copy(gates[:], gates_psum[:])
+
+        entries = [psum.tile([P, D, P], BF16, name="entries_first%d" % h, tag="even%d" % h) for h in range(HALVES)]
+        scaled = keep.tile([P, HALVES, D, P], F32, name="scaled_first", tag="codes0", align_bytes=64)
+        total = [psum.tile([P, P], F32, name="total_first%d" % h, tag="acc%d" % h) for h in range(HALVES)]
+        nc.vector.tensor_copy(picked_first[:], planes[1][0][:].indirect(offsets[:]))
+        for h in range(HALVES):
+            for d in range(D):
+                nc.tensor.transpose(entries[h][:, d, :], picked_first[:, block(d, h)], identity_bf16[:])
+        for h in range(HALVES):
+            for d in range(D):
+                j = HALVES * d + h
+                nc.scalar.activation(scaled[:, h, d, :], entries[h][:, d, :], COPY, scale=gate_cols[:, j : j + 1])
+            add_turned(total[h][:], [scaled[:, h, d, :] for d in range(D)])
+        for h in range(HALVES):
+            nc.scalar.copy(sums[1][:, half(h), 0], total[h][:])
+        last_gates = keep.tile([P, CUT], F32, name="last_gates", tag="codes0", align_bytes=64)
         nc.scalar.copy(last_gates[:], gates_psum[:, 0:CUT])
 
         summed = [psum.tile([P, PACK, P], F32, name="summed%d" % h) for h in range(HALVES)]
@@ -125,27 +140,12 @@ def tile_picked_bag_lin_relu_sub_l_kernel(tc, xT, w_words, w_scales, b, gate, of
         for h in range(HALVES):
             nc.scalar.copy(sums[0][:, half(h), :], summed[h][:].rearrange("p t v -> p v t"))
 
-        turned = [psum.tile([P, PAIR, P], F32, name="turned%d" % h, tag="even%d" % h) for h in range(HALVES)]
-        rounded = [keep.tile([P, P, PAIR], BF16, name="rounded%d" % h) for h in range(HALVES)]
-        words = [psum.tile([P, P], F32, name="words%d" % h, tag="odd%d" % h) for h in range(HALVES)]
-        for e in range(PAIR):
-            nc.vector.tensor_tensor(weighted[0][:, e, :], planes[1][e][:].indirect(offsets[:]), gates[:], MULT)
-            for h in range(HALVES):
-                add_turned(turned[h][:, e, :], [weighted[0][:, e, block(d, h)] for d in range(D)])
-        for h in range(HALVES):
-            nc.scalar.copy(rounded[h][:], turned[h][:].rearrange("v e p -> v p e"))
-        for h in range(HALVES):
-            nc.tensor.transpose(words[h][:], rounded[h][:].rearrange("v p e -> v (p e)").bitcast(F32), identity[:])
-        for h in range(HALVES):
-            nc.scalar.copy(
-                sums[1][:, half(h), 0:PAIR], words[h][:].bitcast(BF16).rearrange("p (v e) -> p v e", e=PAIR)
-            )
-
-        nc.vector.tensor_tensor(weighted[1][:, 0, :], planes[1][PAIR][:].indirect(offsets[:]), gates[:], MULT)
+        for t in range(1, PACK - 1):
+            nc.vector.tensor_tensor(weighted[:, t - 1, :], planes[1][t][:].indirect(offsets[:]), gates[:], MULT)
         parts = ((0, CUT, last_gates[:]), (CUT, S, gates[:, CUT:S]))
         for first, end, factors in parts:
             nc.vector.tensor_tensor(
-                weighted[1][:, 1, first:end],
+                weighted[:, PACK - 2, first:end],
                 planes[1][PACK - 1][:].indirect(offsets[:, first // GROUP : end // GROUP]),
                 factors,
                 MULT,
@@ -156,11 +156,13 @@ def tile_picked_bag_lin_relu_sub_l_kernel(tc, xT, w_words, w_scales, b, gate, of
             keep.tile([P, V], U32, name="x_codes1", align_bytes=64),
         ]
 
+        acc = [psum.tile([P, P], F32, name="acc%d" % h, tag="acc%d" % h) for h in range(HALVES)]
+
         def add_pieces(h):
             nc.vector.tensor_tensor(
-                sums[1][:, half(h), PAIR:PACK].rearrange("p (c i) t -> p c t i", i=RUN),
-                weighted[1][:, :, block(0, h)].rearrange("p t (c i) -> p c t i", i=RUN),
-                weighted[1][:, :, block(1, h)].rearrange("p t (c i) -> p c t i", i=RUN),
+                sums[1][:, half(h), 1:PACK].rearrange("p (c i) t -> p c t i", i=RUN),
+                weighted[:, :, block(0, h)].rearrange("p t (c i) -> p c t i", i=RUN),
+                weighted[:, :, block(1, h)].rearrange("p t (c i) -> p c t i", i=RUN),
                 ADD,
             )
 
@@ -178,18 +180,16 @@ def tile_picked_bag_lin_relu_sub_l_kernel(tc, xT, w_words, w_scales, b, gate, of
                 lhsT_scale=w_scale[:, a, :],
                 rhs=x_codes[a][:, half(h)].bitcast(FP8X4),
                 rhs_scale=x_scale[a][:, half(h)],
-                start=(a == 0),
-                stop=(a == PASSES - 1),
+                start=(a == 1),
+                stop=(a == 0),
             )
 
-        add_pieces(0)
-        quantize(0, slice(0, V))
-        add_pieces(1)
         for h in range(HALVES):
-            multiply(0, h)
+            add_pieces(h)
         for h in range(HALVES):
-            quantize(1, half(h))
-            multiply(1, h)
+            for a in (1, 0):
+                quantize(a, half(h))
+                multiply(a, h)
 
         nc.vector.tensor_scalar(result[0][:], acc[0][:], bias[:], 0.0, ADD, MAX)
         nc.sync.dma_start(out[:, half(0)], result[0][:])

@@ -75,7 +75,8 @@ def tile_picked_bag_lin_relu_sub_l_kernel(tc, xT, w_words, w_scales, b, gate, of
         nc.scalar.activation(relu_of_zero[:], zero[:], RELU)
 
         x_rows = xT.rearrange("(a p t) c -> a t p c", a=PASSES, t=PACK)
-        nc.sync.dma_start(planes[1][0][:], x_rows[1, 0])
+        nc.sync.dma_start(planes[1][0][:, 0 : T // 2], x_rows[1, 0][:, 0 : T // 2])
+        nc.scalar.dma_start(planes[1][0][:, T // 2 : T], x_rows[1, 0][:, T // 2 : T])
         nc.sync.dma_start(offsets[:], offs)
         gate_blocks = gate.rearrange("d r (h v) -> (d r h) v", h=HALVES)
         nc.sync.dma_start(gate_rows[0:BLOCKS, :], gate_blocks[0 : (BLOCKS - 1) * (P + 1) + 1 : P + 1, :])

@@ -50,16 +50,12 @@ def tile_picked_bag_lin_relu_sub_l_kernel(tc, xT, w_words, w_scales, b, gate, of
 
         gate_rows = keep.tile([P, P], F32, name="gate_rows")
         gate_cols = keep.tile([P, BLOCKS], F32, name="gate_cols")
-        gates = keep.tile([P, S], F32, name="gates")
-        gate_cols_psum = psum.tile([P, P], F32, name="gate_cols_psum", tag="odd0")
-        gates_psum = psum.tile([P, S], F32, name="gates_psum", tag="odd1")
+        gate_cols_psum = psum.tile([P, P], F32, name="gate_cols_psum", tag="e3")
+        gates_psum = psum.tile([P, S], F32, name="gates_psum", tag="x")
 
-        picked = [keep.tile([P, S], BF16, name="picked%d" % t) for t in range(PACK)]
-        picked_first = keep.tile([P, S], BF16, name="picked_first")
         weighted = keep.tile([P, PACK - 1, S], F32, name="weighted")
-        sums = [keep.tile([P, V, PACK], BF16, name="sums%d" % a, align_bytes=64) for a in range(PASSES)]
+        sums = [keep.tile([P, V, PACK], BF16, name="sums%d" % a, tag="sums%d" % a, align_bytes=64) for a in range(PASSES)]
         x_scale = [keep.tile([P, V], U8, name="x_scale%d" % a, align_bytes=64) for a in range(PASSES)]
-        result = [keep.tile([P, P], F32, name="result%d" % h) for h in range(HALVES)]
 
         def half(h):
             return slice(h * P, (h + 1) * P)
@@ -67,7 +63,7 @@ def tile_picked_bag_lin_relu_sub_l_kernel(tc, xT, w_words, w_scales, b, gate, of
         def block(d, h):
             return half(HALVES * d + h)
 
-        nc.vector.memset(gate_rows[:], 0.0)
+        nc.gpsimd.memset(gate_rows[:], 0.0)
         nc.vector.memset(zero[:], 0.0)
         nc.vector.memset(w_scale[:].rearrange("p a m -> p (a m)").bitcast(U32), 0)
         make_identity(nc, identity[:])
@@ -75,13 +71,20 @@ def tile_picked_bag_lin_relu_sub_l_kernel(tc, xT, w_words, w_scales, b, gate, of
         nc.scalar.activation(relu_of_zero[:], zero[:], RELU)
 
         x_rows = xT.rearrange("(a p t) c -> a t p c", a=PASSES, t=PACK)
-        nc.sync.dma_start(planes[1][0][:, 0 : T // 2], x_rows[1, 0][:, 0 : T // 2])
-        nc.scalar.dma_start(planes[1][0][:, T // 2 : T], x_rows[1, 0][:, T // 2 : T])
+
+        def load_plane(a, t, split):
+            if split:
+                nc.sync.dma_start(planes[a][t][:, 0 : T // 2], x_rows[a, t][:, 0 : T // 2])
+                nc.scalar.dma_start(planes[a][t][:, T // 2 : T], x_rows[a, t][:, T // 2 : T])
+            else:
+                nc.sync.dma_start(planes[a][t][:], x_rows[a, t])
+
+        load_plane(1, 0, True)
         nc.sync.dma_start(offsets[:], offs)
         gate_blocks = gate.rearrange("d r (h v) -> (d r h) v", h=HALVES)
         nc.sync.dma_start(gate_rows[0:BLOCKS, :], gate_blocks[0 : (BLOCKS - 1) * (P + 1) + 1 : P + 1, :])
         for a, t in [(0, t) for t in range(PACK)] + [(1, t) for t in range(1, PACK)]:
-            nc.sync.dma_start(planes[a][t][:], x_rows[a, t])
+            load_plane(a, t, a == 0 and t < 3)
         nc.sync.dma_start(w_codes[:].bitcast(I32), w_words.rearrange("a p m r -> p a (m r)").bitcast(I32))
         for q in range(QUADRANTS):
             nc.sync.dma_start(
@@ -98,53 +101,55 @@ def tile_picked_bag_lin_relu_sub_l_kernel(tc, xT, w_words, w_scales, b, gate, of
         nc.scalar.copy(gate_cols[:], gate_cols_psum[:, 0:BLOCKS])
         for j in range(BLOCKS):
             nc.tensor.transpose(gates_psum[:, half(j)], gate_cols[:, j : j + 1].to_broadcast([P, P]), identity[:])
+
+        gates = keep.tile([P, S], F32, name="gates")
         nc.scalar.copy(gates[:], gates_psum[:])
 
-        entries = [psum.tile([P, D, P], BF16, name="entries_first%d" % h, tag="even%d" % h) for h in range(HALVES)]
-        scaled = keep.tile([P, HALVES, D, P], F32, name="scaled_first", tag="codes0", align_bytes=64)
-        total = [psum.tile([P, P], F32, name="total_first%d" % h, tag="acc%d" % h) for h in range(HALVES)]
-        nc.vector.tensor_copy(picked_first[:], planes[1][0][:].indirect(offsets[:]))
-        for h in range(HALVES):
-            for d in range(D):
-                nc.tensor.transpose(entries[h][:, d, :], picked_first[:, block(d, h)], identity_bf16[:])
-        for h in range(HALVES):
-            for d in range(D):
-                j = HALVES * d + h
-                nc.scalar.activation(scaled[:, h, d, :], entries[h][:, d, :], COPY, scale=gate_cols[:, j : j + 1])
-            add_turned(total[h][:], [scaled[:, h, d, :] for d in range(D)])
-        for h in range(HALVES):
-            nc.scalar.copy(sums[1][:, half(h), 0], total[h][:])
-        last_gates = keep.tile([P, CUT], F32, name="last_gates", tag="codes0", align_bytes=64)
-        nc.scalar.copy(last_gates[:], gates_psum[:, 0:CUT])
+        def turn(picked, name, tags):
+            banks = [psum.tile([P, HALVES, D, P], BF16, name="entries%s%s" % (name, g), tag=g) for g in tags]
+            for h in range(HALVES):
+                for d in range(D):
+                    nc.tensor.transpose(banks[h % len(tags)][:, h, d, :], picked[:, block(d, h)], identity_bf16[:])
+            return banks
 
-        summed = [psum.tile([P, PACK, P], F32, name="summed%d" % h) for h in range(HALVES)]
-        for u in range(PAIRS):
-            scaled = keep.tile([P, HALVES, D, PAIR, P], F32, name="scaled%d" % u)
-            entries = [
-                psum.tile([P, D, PAIR, P], BF16, name="entries%d%d" % (u, h), tag=("even%d", "odd%d")[u] % h)
-                for h in range(HALVES)
-            ]
-            for e in range(PAIR):
-                t = PAIR * u + e
-                nc.vector.tensor_copy(picked[t][:], planes[0][t][:].indirect(offsets[:]))
-                for h in range(HALVES):
-                    for d in range(D):
-                        nc.tensor.transpose(entries[h][:, d, e, :], picked[t][:, block(d, h)], identity_bf16[:])
+        def gather(a, t, tags):
+            picked = keep.tile([P, S], BF16, name="picked%d%d" % (a, t), tag="picked%d%d" % (a, t))
+            nc.vector.tensor_copy(picked[:], planes[a][t][:].indirect(offsets[:]))
+            return turn(picked, "%d%d" % (a, t), tags)
+
+        def scale(banks, name, total):
+            scaled = keep.tile([P, HALVES, D, P], F32, name="scaled" + name, tag="scaled" + name)
             for h in range(HALVES):
                 for d in range(D):
                     j = HALVES * d + h
                     nc.scalar.activation(
-                        scaled[:, h, d, :, :], entries[h][:, d, :, :], COPY, scale=gate_cols[:, j : j + 1]
+                        scaled[:, h, d, :], banks[h % len(banks)][:, h, d, :], COPY, scale=gate_cols[:, j : j + 1]
                     )
-                for e in range(PAIR):
-                    add_turned(summed[h][:, PAIR * u + e, :], [scaled[:, h, d, e, :] for d in range(D)])
+                add_turned(total(h), [scaled[:, h, d, :] for d in range(D)])
+
+        summed1 = psum.tile([P, V], F32, name="summed1")
+        summed0 = [psum.tile([P, PACK, P], F32, name="summed0%d" % h) for h in range(HALVES)]
+        scale(gather(1, 0, ["e0"]), "10", lambda h: summed1[:, half(h)])
+        banks00 = gather(0, 0, ["e1"])
+        narrow = keep.tile([P, T], BF16, name="narrow")
+        nc.vector.tensor_copy(narrow[:], planes[0][1][:])
+        picked01 = keep.tile([P, S], BF16, name="picked01", tag="picked10")
+        nc.scalar.activation(picked01[:], narrow[:].indirect(offsets[:]), COPY)
+        scale(banks00, "00", lambda h: summed0[h][:, 0, :])
+        banks01 = turn(picked01, "01", ["e2"])
+        nc.scalar.copy(sums[1][:, :, 0], summed1[:])
+        last_gates = keep.tile([P, S - CUT], F32, name="last_gates", tag="scaled10")
+        nc.scalar.copy(last_gates[:], gates[:, CUT:S])
+        banks02 = gather(0, 2, ["e3"])
+        scale(banks02, "02", lambda h: summed0[h][:, 2, :])
+        scale(banks01, "01", lambda h: summed0[h][:, 1, :])
+        scale(gather(0, 3, ["e0", "e1"]), "03", lambda h: summed0[h][:, 3, :])
         for h in range(HALVES):
-            nc.scalar.copy(sums[0][:, half(h), :], summed[h][:].rearrange("p t v -> p v t"))
+            nc.scalar.copy(sums[0][:, half(h), :], summed0[h][:].rearrange("p t v -> p v t"))
 
         for t in range(1, PACK - 1):
             nc.vector.tensor_tensor(weighted[:, t - 1, :], planes[1][t][:].indirect(offsets[:]), gates[:], MULT)
-        parts = ((0, CUT, last_gates[:]), (CUT, S, gates[:, CUT:S]))
-        for first, end, factors in parts:
+        for first, end, factors in ((0, CUT, gates[:, 0:CUT]), (CUT, S, last_gates[:])):
             nc.vector.tensor_tensor(
                 weighted[:, PACK - 2, first:end],
                 planes[1][PACK - 1][:].indirect(offsets[:, first // GROUP : end // GROUP]),
@@ -152,12 +157,8 @@ def tile_picked_bag_lin_relu_sub_l_kernel(tc, xT, w_words, w_scales, b, gate, of
                 MULT,
             )
 
-        x_codes = [
-            keep.tile([P, V], U32, name="x_codes0", tag="codes0", align_bytes=64),
-            keep.tile([P, V], U32, name="x_codes1", align_bytes=64),
-        ]
-
-        acc = [psum.tile([P, P], F32, name="acc%d" % h, tag="acc%d" % h) for h in range(HALVES)]
+        x_codes = [keep.tile([P, V], U32, name="x_codes%d" % a, align_bytes=64) for a in range(PASSES)]
+        acc = [psum.tile([P, P], F32, name="acc%d" % h, tag=("e2", "x")[h]) for h in range(HALVES)]
 
         def add_pieces(h):
             nc.vector.tensor_tensor(
@@ -192,6 +193,10 @@ def tile_picked_bag_lin_relu_sub_l_kernel(tc, xT, w_words, w_scales, b, gate, of
                 quantize(a, half(h))
                 multiply(a, h)
 
+        result = [
+            keep.tile([P, P], F32, name="result0", tag="sums0", align_bytes=64),
+            keep.tile([P, P], F32, name="result1"),
+        ]
         nc.vector.tensor_scalar(result[0][:], acc[0][:], bias[:], 0.0, ADD, MAX)
         nc.sync.dma_start(out[:, half(0)], result[0][:])
         nc.scalar.activation(result[1][:], acc[1][:], RELU, bias=bias[:])

@@ -84,7 +84,7 @@ def tile_picked_bag_lin_relu_sub_l_kernel(tc, xT, w_words, w_scales, b, gate, of
         gate_blocks = gate.rearrange("d r (h v) -> (d r h) v", h=HALVES)
         nc.sync.dma_start(gate_rows[0:BLOCKS, :], gate_blocks[0 : (BLOCKS - 1) * (P + 1) + 1 : P + 1, :])
         for a, t in [(0, t) for t in range(PACK)] + [(1, t) for t in range(1, PACK)]:
-            load_plane(a, t, a == 0 and t < 3)
+            load_plane(a, t, a == 0 and t < 0)
         nc.sync.dma_start(w_codes[:].bitcast(I32), w_words.rearrange("a p m r -> p a (m r)").bitcast(I32))
         for q in range(QUADRANTS):
             nc.sync.dma_start(

@@ -131,31 +131,26 @@ def tile_picked_bag_lin_relu_sub_l_kernel(tc, xT, w_words, w_scales, b, gate, of
         summed0 = [psum.tile([P, PACK, P], F32, name="summed0%d" % h) for h in range(HALVES)]
         scale(gather(1, 0, ["e0"]), "10", lambda h: summed1[:, half(h)])
         banks00 = gather(0, 0, ["e1"])
-        narrow = keep.tile([P, T], BF16, name="narrow")
-        nc.vector.tensor_copy(narrow[:], planes[0][1][:])
         picked01 = keep.tile([P, S], BF16, name="picked01", tag="picked10")
-        nc.scalar.activation(picked01[:], narrow[:].indirect(offsets[:]), COPY)
+        nc.scalar.activation(picked01[:], planes[0][1][:].indirect(offsets[:]), COPY)
         scale(banks00, "00", lambda h: summed0[h][:, 0, :])
         banks01 = turn(picked01, "01", ["e2"])
         nc.scalar.copy(sums[1][:, :, 0], summed1[:])
-        last_gates = keep.tile([P, S - CUT], F32, name="last_gates", tag="scaled10")
-        nc.scalar.copy(last_gates[:], gates[:, CUT:S])
         banks02 = gather(0, 2, ["e3"])
         scale(banks02, "02", lambda h: summed0[h][:, 2, :])
         scale(banks01, "01", lambda h: summed0[h][:, 1, :])
         scale(gather(0, 3, ["e0", "e1"]), "03", lambda h: summed0[h][:, 3, :])
+        last = keep.tile([P, HALVES, P], F32, name="last", tag="picked03")
+        nc.scalar.activation(last[:, 0, :], planes[1][PACK - 1][:].indirect(offsets[:, V // GROUP : CUT // GROUP]), COPY)
+        nc.scalar.activation(last[:, 1, :], planes[1][PACK - 1][:].indirect(offsets[:, CUT // GROUP : S // GROUP]), COPY)
         for h in range(HALVES):
             nc.scalar.copy(sums[0][:, half(h), :], summed0[h][:].rearrange("p t v -> p v t"))
 
         for t in range(1, PACK - 1):
             nc.vector.tensor_tensor(weighted[:, t - 1, :], planes[1][t][:].indirect(offsets[:]), gates[:], MULT)
-        for first, end, factors in ((0, CUT, gates[:, 0:CUT]), (CUT, S, last_gates[:])):
-            nc.vector.tensor_tensor(
-                weighted[:, PACK - 2, first:end],
-                planes[1][PACK - 1][:].indirect(offsets[:, first // GROUP : end // GROUP]),
-                factors,
-                MULT,
-            )
+        nc.vector.tensor_tensor(weighted[:, PACK - 2, 0:V], planes[1][PACK - 1][:].indirect(offsets[:, 0 : V // GROUP]), gates[:, 0:V], MULT)
+        nc.vector.tensor_tensor(weighted[:, PACK - 2, V:CUT], last[:, 0, :], gates[:, V:CUT], MULT)
+        nc.vector.tensor_tensor(weighted[:, PACK - 2, CUT:S], last[:, 1, :], gates[:, CUT:S], MULT)
 
         x_codes = [keep.tile([P, V], U32, name="x_codes%d" % a, align_bytes=64) for a in range(PASSES)]
         acc = [psum.tile([P, P], F32, name="acc%d" % h, tag=("e2", "x")[h]) for h in range(HALVES)]

@@ -39,7 +39,10 @@ def tile_picked_bag_lin_relu_sub_l_kernel(tc, xT, w_words, w_scales, b, gate, of
         psum = ctx.enter_context(tc.psum_pool(name="psum", bufs=1))
 
         offsets = keep.tile([P, S // GROUP], U16, name="offsets")
-        planes = [[keep.tile([P, T], F32, name="plane%d%d" % (a, t)) for t in range(PACK)] for a in range(PASSES)]
+        planes = [
+            [keep.tile([P, T], F32, name="plane%d%d" % (a, t), tag="sums0" if (a, t) == (1, 3) else "plane%d%d" % (a, t), align_bytes=64) for t in range(PACK)]
+            for a in range(PASSES)
+        ]
         w_codes = keep.tile([P, PASSES, N * PACK], U8, name="w_codes", align_bytes=64)
         w_scale = keep.tile([P, PASSES, N], U8, name="w_scale", align_bytes=64)
         bias = keep.tile([P, 1], F32, name="bias")
@@ -50,10 +53,10 @@ def tile_picked_bag_lin_relu_sub_l_kernel(tc, xT, w_words, w_scales, b, gate, of
 
         gate_rows = keep.tile([P, P], F32, name="gate_rows")
         gate_cols = keep.tile([P, BLOCKS], F32, name="gate_cols")
-        gate_cols_psum = psum.tile([P, P], F32, name="gate_cols_psum", tag="e3")
+        gate_cols_psum = psum.tile([P, P], F32, name="gate_cols_psum", tag="e2")
         gates_psum = psum.tile([P, S], F32, name="gates_psum", tag="x")
 
-        weighted = keep.tile([P, PACK - 1, S], F32, name="weighted")
+        weighted = keep.tile([P, PACK - 1, S], F32, name="weighted", tag="picked01")
         sums = [keep.tile([P, V, PACK], BF16, name="sums%d" % a, tag="sums%d" % a, align_bytes=64) for a in range(PASSES)]
         x_scale = [keep.tile([P, V], U8, name="x_scale%d" % a, align_bytes=64) for a in range(PASSES)]
 
@@ -99,11 +102,6 @@ def tile_picked_bag_lin_relu_sub_l_kernel(tc, xT, w_words, w_scales, b, gate, of
 
         nc.tensor.transpose(gate_cols_psum[:], gate_rows[:], identity[:])
         nc.scalar.copy(gate_cols[:], gate_cols_psum[:, 0:BLOCKS])
-        for j in range(BLOCKS):
-            nc.tensor.transpose(gates_psum[:, half(j)], gate_cols[:, j : j + 1].to_broadcast([P, P]), identity[:])
-
-        gates = keep.tile([P, S], F32, name="gates")
-        nc.scalar.copy(gates[:], gates_psum[:])
 
         def turn(picked, name, tags):
             banks = [psum.tile([P, HALVES, D, P], BF16, name="entries%s%s" % (name, g), tag=g) for g in tags]
@@ -112,35 +110,43 @@ def tile_picked_bag_lin_relu_sub_l_kernel(tc, xT, w_words, w_scales, b, gate, of
                     nc.tensor.transpose(banks[h % len(tags)][:, h, d, :], picked[:, block(d, h)], identity_bf16[:])
             return banks
 
-        def gather(a, t, tags):
-            picked = keep.tile([P, S], BF16, name="picked%d%d" % (a, t), tag="picked%d%d" % (a, t))
+        def gather(a, t, tags, tag):
+            picked = keep.tile([P, S], BF16, name="picked%d%d" % (a, t), tag=tag)
             nc.vector.tensor_copy(picked[:], planes[a][t][:].indirect(offsets[:]))
             return turn(picked, "%d%d" % (a, t), tags)
 
         def scale(banks, name, total):
-            scaled = keep.tile([P, HALVES, D, P], F32, name="scaled" + name, tag="scaled" + name)
             for h in range(HALVES):
+                scaled = keep.tile([P, D, P], F32, name="scaled%s%d" % (name, h), tag="scaled%s%d" % (name, h))
                 for d in range(D):
                     j = HALVES * d + h
                     nc.scalar.activation(
-                        scaled[:, h, d, :], banks[h % len(banks)][:, h, d, :], COPY, scale=gate_cols[:, j : j + 1]
+                        scaled[:, d, :], banks[h % len(banks)][:, h, d, :], COPY, scale=gate_cols[:, j : j + 1]
                     )
-                add_turned(total(h), [scaled[:, h, d, :] for d in range(D)])
+                add_turned(total(h), [scaled[:, d, :] for d in range(D)])
 
-        summed1 = psum.tile([P, V], F32, name="summed1")
+        summed1 = [psum.tile([P, P], F32, name="summed1%d" % h) for h in range(HALVES)]
         summed0 = [psum.tile([P, PACK, P], F32, name="summed0%d" % h) for h in range(HALVES)]
-        scale(gather(1, 0, ["e0"]), "10", lambda h: summed1[:, half(h)])
-        banks00 = gather(0, 0, ["e1"])
-        picked01 = keep.tile([P, S], BF16, name="picked01", tag="picked10")
-        nc.scalar.activation(picked01[:], planes[0][1][:].indirect(offsets[:]), COPY)
+        banks10 = gather(1, 0, ["e0"], "picked10")
+        for j in range(BLOCKS):
+            nc.tensor.transpose(gates_psum[:, half(j)], gate_cols[:, j : j + 1].to_broadcast([P, P]), identity[:])
+
+        scale(banks10, "10", lambda h: summed1[h][:])
+        gates = keep.tile([P, S], F32, name="gates")
+        nc.scalar.copy(gates[:], gates_psum[:])
+        banks00 = gather(0, 0, ["e0"], "picked00")
+        banks01 = gather(0, 1, ["x"], "picked01")
+        for h in range(HALVES):
+            nc.vector.tensor_copy(sums[1][:, half(h), 0], summed1[h][:])
+        picked02 = keep.tile([P, S], BF16, name="picked02", tag="scaled100")
+        nc.scalar.activation(picked02[:], planes[0][2][:].indirect(offsets[:]), COPY)
         scale(banks00, "00", lambda h: summed0[h][:, 0, :])
-        banks01 = turn(picked01, "01", ["e2"])
-        nc.scalar.copy(sums[1][:, :, 0], summed1[:])
-        banks02 = gather(0, 2, ["e3"])
-        scale(banks02, "02", lambda h: summed0[h][:, 2, :])
+        banks02 = turn(picked02, "02", ["e2"])
+        banks03 = gather(0, 3, ["e0"], "scaled101")
         scale(banks01, "01", lambda h: summed0[h][:, 1, :])
-        scale(gather(0, 3, ["e0", "e1"]), "03", lambda h: summed0[h][:, 3, :])
-        last = keep.tile([P, HALVES, P], F32, name="last", tag="picked03")
+        scale(banks02, "02", lambda h: summed0[h][:, 2, :])
+        scale(banks03, "03", lambda h: summed0[h][:, 3, :])
+        last = keep.tile([P, HALVES, P], F32, name="last", tag="scaled101")
         nc.scalar.activation(last[:, 0, :], planes[1][PACK - 1][:].indirect(offsets[:, V // GROUP : CUT // GROUP]), COPY)
         nc.scalar.activation(last[:, 1, :], planes[1][PACK - 1][:].indirect(offsets[:, CUT // GROUP : S // GROUP]), COPY)
         for h in range(HALVES):

@@ -77,8 +77,8 @@ def tile_picked_bag_lin_relu_sub_l_kernel(tc, xT, w_words, w_scales, b, gate, of
 
         def load_plane(a, t, split):
             if split:
-                nc.sync.dma_start(planes[a][t][:, 0 : T // 2], x_rows[a, t][:, 0 : T // 2])
-                nc.scalar.dma_start(planes[a][t][:, T // 2 : T], x_rows[a, t][:, T // 2 : T])
+                nc.sync.dma_start(planes[a][t][:, 0 : T // 4], x_rows[a, t][:, 0 : T // 4])
+                nc.scalar.dma_start(planes[a][t][:, T // 4 : T], x_rows[a, t][:, T // 4 : T])
             else:
                 nc.sync.dma_start(planes[a][t][:], x_rows[a, t])
 

@@ -56,12 +56,17 @@ def tile_picked_bag_lin_relu_sub_l_kernel(tc, xT, w_words, w_scales, b, gate, of
         gate_cols_psum = psum.tile([P, P], F32, name="gate_cols_psum", tag="e2")
         gates_psum = psum.tile([P, S], F32, name="gates_psum", tag="x")
 
-        weighted = keep.tile([P, PACK - 1, S], F32, name="weighted", tag="picked01")
         sums = [keep.tile([P, V, PACK], BF16, name="sums%d" % a, tag="sums%d" % a, align_bytes=64) for a in range(PASSES)]
         x_scale = [keep.tile([P, V], U8, name="x_scale%d" % a, align_bytes=64) for a in range(PASSES)]
 
         def half(h):
             return slice(h * P, (h + 1) * P)
+
+        def piece(d):
+            return slice(d * V, (d + 1) * V)
+
+        def entries(d):
+            return offsets[:, d * V // GROUP : (d + 1) * V // GROUP]
 
         def block(d, h):
             return half(HALVES * d + h)
@@ -82,12 +87,12 @@ def tile_picked_bag_lin_relu_sub_l_kernel(tc, xT, w_words, w_scales, b, gate, of
             else:
                 nc.sync.dma_start(planes[a][t][:], x_rows[a, t])
 
-        load_plane(1, 0, True)
+        load_plane(0, 0, True)
         nc.sync.dma_start(offsets[:], offs)
         gate_blocks = gate.rearrange("d r (h v) -> (d r h) v", h=HALVES)
         nc.sync.dma_start(gate_rows[0:BLOCKS, :], gate_blocks[0 : (BLOCKS - 1) * (P + 1) + 1 : P + 1, :])
-        for a, t in [(0, t) for t in range(PACK)] + [(1, t) for t in range(1, PACK)]:
-            load_plane(a, t, a == 0 and t < 0)
+        for a, t in [(0, 1), (0, 2), (1, 0), (0, 3)] + [(1, t) for t in range(1, PACK)]:
+            load_plane(a, t, False)
         nc.sync.dma_start(w_codes[:].bitcast(I32), w_words.rearrange("a p m r -> p a (m r)").bitcast(I32))
         for q in range(QUADRANTS):
             nc.sync.dma_start(
@@ -125,28 +130,45 @@ def tile_picked_bag_lin_relu_sub_l_kernel(tc, xT, w_words, w_scales, b, gate, of
                     )
                 add_turned(total(h), [scaled[:, d, :] for d in range(D)])
 
-        summed1 = [psum.tile([P, P], F32, name="summed1%d" % h) for h in range(HALVES)]
         summed0 = [psum.tile([P, PACK, P], F32, name="summed0%d" % h) for h in range(HALVES)]
-        banks10 = gather(1, 0, ["e0"], "picked10")
+        picked00 = keep.tile([P, S], BF16, name="picked00")
+        nc.vector.tensor_copy(picked00[:, piece(0)], planes[0][0][:].indirect(entries(0)))
+        nc.scalar.activation(picked00[:, piece(1)], planes[0][0][:].indirect(entries(1)), COPY)
+        banks00 = turn(picked00, "00", ["e0"])
         for j in range(BLOCKS):
             nc.tensor.transpose(gates_psum[:, half(j)], gate_cols[:, j : j + 1].to_broadcast([P, P]), identity[:])
 
-        scale(banks10, "10", lambda h: summed1[h][:])
-        gates = keep.tile([P, S], F32, name="gates")
-        nc.scalar.copy(gates[:], gates_psum[:])
-        banks00 = gather(0, 0, ["e0"], "picked00")
-        banks01 = gather(0, 1, ["x"], "picked01")
-        for h in range(HALVES):
-            nc.vector.tensor_copy(sums[1][:, half(h), 0], summed1[h][:])
-        picked02 = keep.tile([P, S], BF16, name="picked02", tag="scaled100")
-        nc.scalar.activation(picked02[:], planes[0][2][:].indirect(offsets[:]), COPY)
         scale(banks00, "00", lambda h: summed0[h][:, 0, :])
-        banks02 = turn(picked02, "02", ["e2"])
-        banks03 = gather(0, 3, ["e0"], "scaled101")
+        gates = keep.tile([P, S], F32, name="gates")
+        for d in range(D):
+            nc.scalar.copy(gates[:, piece(d)], gates_psum[:, piece(d)])
+        banks01 = gather(0, 1, ["e0"], "picked01")
+        banks02 = gather(0, 2, ["x"], "picked02")
+        early = keep.tile([P, S], F32, name="early")
+        for first, end in ((0, V), (V, CUT), (CUT, S)):
+            nc.vector.tensor_tensor(
+                early[:, first:end], planes[1][0][:].indirect(offsets[:, first // GROUP : end // GROUP]), gates[:, first:end], MULT
+            )
+        for h in range(HALVES):
+            nc.vector.tensor_tensor(sums[1][:, half(h), 0], early[:, block(0, h)], early[:, block(1, h)], ADD)
         scale(banks01, "01", lambda h: summed0[h][:, 1, :])
+
+        picked03 = keep.tile([P, S], BF16, name="picked03", tag="picked01")
+        banks03 = [psum.tile([P, HALVES, P], BF16, name="entries03%d" % d, tag=("e0", "e2")[d]) for d in range(D)]
+        for d in range(D):
+            nc.scalar.activation(picked03[:, piece(d)], planes[0][3][:].indirect(entries(d)), COPY)
+            for h in range(HALVES):
+                nc.tensor.transpose(banks03[d][:, h, :], picked03[:, block(d, h)], identity_bf16[:])
         scale(banks02, "02", lambda h: summed0[h][:, 2, :])
-        scale(banks03, "03", lambda h: summed0[h][:, 3, :])
-        last = keep.tile([P, HALVES, P], F32, name="last", tag="scaled101")
+        scaled03 = [keep.tile([P, D, P], F32, name="scaled03%d" % h) for h in range(HALVES)]
+        for d in range(D):
+            for h in range(HALVES):
+                j = HALVES * d + h
+                nc.scalar.activation(scaled03[h][:, d, :], banks03[d][:, h, :], COPY, scale=gate_cols[:, j : j + 1])
+        for h in range(HALVES):
+            add_turned(summed0[h][:, 3, :], [scaled03[h][:, d, :] for d in range(D)])
+        weighted = keep.tile([P, PACK - 1, S], F32, name="weighted", tag="scaled010")
+        last = keep.tile([P, HALVES, P], F32, name="last", tag="picked01")
         nc.scalar.activation(last[:, 0, :], planes[1][PACK - 1][:].indirect(offsets[:, V // GROUP : CUT // GROUP]), COPY)
         nc.scalar.activation(last[:, 1, :], planes[1][PACK - 1][:].indirect(offsets[:, CUT // GROUP : S // GROUP]), COPY)
         for h in range(HALVES):

@@ -7,15 +7,15 @@ K, T, D, V, N = 1024, 1024, 2, 256, 128
 S = D * V
 P = 128
 PACK = 4
+LAST = PACK - 1
 PASSES = K // (P * PACK)
 HALVES = V // P
 BLOCKS = S // P
 QUADRANTS = 4
-PAIR = 2
-PAIRS = PACK // PAIR
 GROUP = 16
 CUT = S - P
 RUN = 2
+SYNC_SHARE = T // 4
 FLOPS = 2 * K * V * N
 
 F32 = mybir.dt.float32
@@ -38,9 +38,12 @@ def tile_picked_bag_lin_relu_sub_l_kernel(tc, xT, w_words, w_scales, b, gate, of
         keep = ctx.enter_context(tc.tile_pool(name="keep", bufs=1))
         psum = ctx.enter_context(tc.psum_pool(name="psum", bufs=1))
 
+        def plane_tag(a, t):
+            return "sums0" if (a, t) == (1, LAST) else "plane%d%d" % (a, t)
+
         offsets = keep.tile([P, S // GROUP], U16, name="offsets")
         planes = [
-            [keep.tile([P, T], F32, name="plane%d%d" % (a, t), tag="sums0" if (a, t) == (1, 3) else "plane%d%d" % (a, t), align_bytes=64) for t in range(PACK)]
+            [keep.tile([P, T], F32, name="plane%d%d" % (a, t), tag=plane_tag(a, t), align_bytes=64) for t in range(PACK)]
             for a in range(PASSES)
         ]
         w_codes = keep.tile([P, PASSES, N * PACK], U8, name="w_codes", align_bytes=64)
@@ -53,8 +56,9 @@ def tile_picked_bag_lin_relu_sub_l_kernel(tc, xT, w_words, w_scales, b, gate, of
 
         gate_rows = keep.tile([P, P], F32, name="gate_rows")
         gate_cols = keep.tile([P, BLOCKS], F32, name="gate_cols")
-        gate_cols_psum = psum.tile([P, P], F32, name="gate_cols_psum", tag="e2")
-        gates_psum = psum.tile([P, S], F32, name="gates_psum", tag="x")
+        gate_cols_psum = psum.tile([P, P], F32, name="gate_cols_psum", tag="bank_a")
+        gates_psum = [psum.tile([P, V], BF16, name="gates_psum%d" % d, tag=("bank_c", "bank_b")[d]) for d in range(D)]
+        gate_cols_bf16 = keep.tile([P, BLOCKS], BF16, name="gate_cols_bf16")
 
         sums = [keep.tile([P, V, PACK], BF16, name="sums%d" % a, tag="sums%d" % a, align_bytes=64) for a in range(PASSES)]
         x_scale = [keep.tile([P, V], U8, name="x_scale%d" % a, align_bytes=64) for a in range(PASSES)]
@@ -65,11 +69,13 @@ def tile_picked_bag_lin_relu_sub_l_kernel(tc, xT, w_words, w_scales, b, gate, of
         def piece(d):
             return slice(d * V, (d + 1) * V)
 
-        def entries(d):
-            return offsets[:, d * V // GROUP : (d + 1) * V // GROUP]
-
         def block(d, h):
             return half(HALVES * d + h)
+
+        def window(a, t, entries):
+            return planes[a][t][:].indirect(offsets[:, entries.start // GROUP : entries.stop // GROUP])
+
+        whole = slice(0, S)
 
         nc.gpsimd.memset(gate_rows[:], 0.0)
         nc.vector.memset(zero[:], 0.0)
@@ -79,20 +85,13 @@ def tile_picked_bag_lin_relu_sub_l_kernel(tc, xT, w_words, w_scales, b, gate, of
         nc.scalar.activation(relu_of_zero[:], zero[:], RELU)
 
         x_rows = xT.rearrange("(a p t) c -> a t p c", a=PASSES, t=PACK)
-
-        def load_plane(a, t, split):
-            if split:
-                nc.sync.dma_start(planes[a][t][:, 0 : T // 4], x_rows[a, t][:, 0 : T // 4])
-                nc.scalar.dma_start(planes[a][t][:, T // 4 : T], x_rows[a, t][:, T // 4 : T])
-            else:
-                nc.sync.dma_start(planes[a][t][:], x_rows[a, t])
-
-        load_plane(0, 0, True)
+        nc.sync.dma_start(planes[0][0][:, 0:SYNC_SHARE], x_rows[0, 0][:, 0:SYNC_SHARE])
+        nc.scalar.dma_start(planes[0][0][:, SYNC_SHARE:T], x_rows[0, 0][:, SYNC_SHARE:T])
         nc.sync.dma_start(offsets[:], offs)
         gate_blocks = gate.rearrange("d r (h v) -> (d r h) v", h=HALVES)
         nc.sync.dma_start(gate_rows[0:BLOCKS, :], gate_blocks[0 : (BLOCKS - 1) * (P + 1) + 1 : P + 1, :])
-        for a, t in [(0, 1), (0, 2), (1, 0), (0, 3)] + [(1, t) for t in range(1, PACK)]:
-            load_plane(a, t, False)
+        for a, t in [(0, 1), (0, 2), (1, 0), (0, LAST)] + [(1, t) for t in range(1, PACK)]:
+            nc.sync.dma_start(planes[a][t][:], x_rows[a, t])
         nc.sync.dma_start(w_codes[:].bitcast(I32), w_words.rearrange("a p m r -> p a (m r)").bitcast(I32))
         for q in range(QUADRANTS):
             nc.sync.dma_start(
@@ -106,115 +105,113 @@ def tile_picked_bag_lin_relu_sub_l_kernel(tc, xT, w_words, w_scales, b, gate, of
                 nc.tensor.matmul(total, parts[d], identity[:], start=(d == 0), stop=(d == D - 1), is_transpose=True)
 
         nc.tensor.transpose(gate_cols_psum[:], gate_rows[:], identity[:])
+        nc.scalar.copy(gate_cols_bf16[:], gate_cols_psum[:, 0:BLOCKS])
         nc.scalar.copy(gate_cols[:], gate_cols_psum[:, 0:BLOCKS])
 
-        def turn(picked, name, tags):
-            banks = [psum.tile([P, HALVES, D, P], BF16, name="entries%s%s" % (name, g), tag=g) for g in tags]
+        def turn(picked, t, tag):
+            bank = psum.tile([P, HALVES, D, P], BF16, name="entries%d" % t, tag=tag)
             for h in range(HALVES):
                 for d in range(D):
-                    nc.tensor.transpose(banks[h % len(tags)][:, h, d, :], picked[:, block(d, h)], identity_bf16[:])
-            return banks
+                    nc.tensor.transpose(bank[:, h, d, :], picked[:, block(d, h)], identity_bf16[:])
+            return bank
 
-        def gather(a, t, tags, tag):
-            picked = keep.tile([P, S], BF16, name="picked%d%d" % (a, t), tag=tag)
-            nc.vector.tensor_copy(picked[:], planes[a][t][:].indirect(offsets[:]))
-            return turn(picked, "%d%d" % (a, t), tags)
+        def gather(t, tag):
+            picked = keep.tile([P, S], BF16, name="picked%d" % t, tag="picked%d" % t)
+            nc.vector.tensor_copy(picked[:], window(0, t, whole))
+            return turn(picked, t, tag)
 
-        def scale(banks, name, total):
+        def scale(product, turned, d, h):
+            j = HALVES * d + h
+            nc.scalar.activation(product, turned, COPY, scale=gate_cols[:, j : j + 1])
+
+        def scale_and_sum(bank, t):
             for h in range(HALVES):
-                scaled = keep.tile([P, D, P], F32, name="scaled%s%d" % (name, h), tag="scaled%s%d" % (name, h))
+                scaled = keep.tile([P, D, P], F32, name="scaled%d%d" % (t, h), tag="scaled%d%d" % (t, h))
                 for d in range(D):
-                    j = HALVES * d + h
-                    nc.scalar.activation(
-                        scaled[:, d, :], banks[h % len(banks)][:, h, d, :], COPY, scale=gate_cols[:, j : j + 1]
-                    )
-                add_turned(total(h), [scaled[:, d, :] for d in range(D)])
+                    scale(scaled[:, d, :], bank[:, h, d, :], d, h)
+                add_turned(summed0[h][:, t, :], [scaled[:, d, :] for d in range(D)])
 
         summed0 = [psum.tile([P, PACK, P], F32, name="summed0%d" % h) for h in range(HALVES)]
-        picked00 = keep.tile([P, S], BF16, name="picked00")
-        nc.vector.tensor_copy(picked00[:, piece(0)], planes[0][0][:].indirect(entries(0)))
-        nc.scalar.activation(picked00[:, piece(1)], planes[0][0][:].indirect(entries(1)), COPY)
-        banks00 = turn(picked00, "00", ["e0"])
-        for j in range(BLOCKS):
-            nc.tensor.transpose(gates_psum[:, half(j)], gate_cols[:, j : j + 1].to_broadcast([P, P]), identity[:])
 
-        scale(banks00, "00", lambda h: summed0[h][:, 0, :])
+        picked0 = keep.tile([P, S], BF16, name="picked0")
+        nc.vector.tensor_copy(picked0[:, piece(0)], window(0, 0, piece(0)))
+        nc.scalar.activation(picked0[:, piece(1)], window(0, 0, piece(1)), COPY)
         gates = keep.tile([P, S], F32, name="gates")
-        for d in range(D):
-            nc.scalar.copy(gates[:, piece(d)], gates_psum[:, piece(d)])
-        banks01 = gather(0, 1, ["e0"], "picked01")
-        banks02 = gather(0, 2, ["x"], "picked02")
-        early = keep.tile([P, S], F32, name="early")
-        for first, end in ((0, V), (V, CUT), (CUT, S)):
-            nc.vector.tensor_tensor(
-                early[:, first:end], planes[1][0][:].indirect(offsets[:, first // GROUP : end // GROUP]), gates[:, first:end], MULT
-            )
-        for h in range(HALVES):
-            nc.vector.tensor_tensor(sums[1][:, half(h), 0], early[:, block(0, h)], early[:, block(1, h)], ADD)
-        scale(banks01, "01", lambda h: summed0[h][:, 1, :])
-
-        picked03 = keep.tile([P, S], BF16, name="picked03", tag="picked01")
-        banks03 = [psum.tile([P, HALVES, P], BF16, name="entries03%d" % d, tag=("e0", "e2")[d]) for d in range(D)]
-        for d in range(D):
-            nc.scalar.activation(picked03[:, piece(d)], planes[0][3][:].indirect(entries(d)), COPY)
-            for h in range(HALVES):
-                nc.tensor.transpose(banks03[d][:, h, :], picked03[:, block(d, h)], identity_bf16[:])
-        scale(banks02, "02", lambda h: summed0[h][:, 2, :])
-        scaled03 = [keep.tile([P, D, P], F32, name="scaled03%d" % h) for h in range(HALVES)]
         for d in range(D):
             for h in range(HALVES):
                 j = HALVES * d + h
-                nc.scalar.activation(scaled03[h][:, d, :], banks03[d][:, h, :], COPY, scale=gate_cols[:, j : j + 1])
+                column = gate_cols_bf16[:, j : j + 1].to_broadcast([P, P])
+                nc.tensor.transpose(gates_psum[d][:, half(h)], column, identity_bf16[:])
+            nc.scalar.copy(gates[:, piece(d)], gates_psum[d][:])
+        bank0 = turn(picked0, 0, "bank_a")
+        bank1 = gather(1, "bank_c")
+        scale_and_sum(bank0, 0)
+        bank2 = gather(2, "bank_a")
+
+        first_products = keep.tile([P, S], F32, name="first_products")
+        for entries in (piece(0), slice(V, CUT), slice(CUT, S)):
+            nc.vector.tensor_tensor(first_products[:, entries], window(1, 0, entries), gates[:, entries], MULT)
         for h in range(HALVES):
-            add_turned(summed0[h][:, 3, :], [scaled03[h][:, d, :] for d in range(D)])
-        weighted = keep.tile([P, PACK - 1, S], F32, name="weighted", tag="scaled010")
-        last = keep.tile([P, HALVES, P], F32, name="last", tag="picked01")
-        nc.scalar.activation(last[:, 0, :], planes[1][PACK - 1][:].indirect(offsets[:, V // GROUP : CUT // GROUP]), COPY)
-        nc.scalar.activation(last[:, 1, :], planes[1][PACK - 1][:].indirect(offsets[:, CUT // GROUP : S // GROUP]), COPY)
+            nc.vector.tensor_tensor(
+                sums[1][:, half(h), 0], first_products[:, block(0, h)], first_products[:, block(1, h)], ADD
+            )
+        scale_and_sum(bank1, 1)
+
+        picked3 = keep.tile([P, S], BF16, name="picked3", tag="picked1")
+        banks3 = [
+            psum.tile([P, HALVES, P], BF16, name="entries3%d" % d, tag=("bank_c", "bank_b")[d]) for d in range(D)
+        ]
+        for d in range(D):
+            nc.scalar.activation(picked3[:, piece(d)], window(0, LAST, piece(d)), COPY)
+            for h in range(HALVES):
+                nc.tensor.transpose(banks3[d][:, h, :], picked3[:, block(d, h)], identity_bf16[:])
+        scale_and_sum(bank2, 2)
+        scaled3 = [keep.tile([P, D, P], F32, name="scaled3%d" % h) for h in range(HALVES)]
+        for d in range(D):
+            for h in range(HALVES):
+                scale(scaled3[h][:, d, :], banks3[d][:, h, :], d, h)
+        for h in range(HALVES):
+            add_turned(summed0[h][:, LAST, :], [scaled3[h][:, d, :] for d in range(D)])
+
+        weighted = keep.tile([P, PACK - 1, S], F32, name="weighted", tag="scaled10")
+        shared = keep.tile([P, HALVES, P], F32, name="shared", tag="picked1")
+        for h in range(HALVES):
+            nc.scalar.activation(shared[:, h, :], window(1, LAST, block(1, h)), COPY)
         for h in range(HALVES):
             nc.scalar.copy(sums[0][:, half(h), :], summed0[h][:].rearrange("p t v -> p v t"))
 
-        for t in range(1, PACK - 1):
-            nc.vector.tensor_tensor(weighted[:, t - 1, :], planes[1][t][:].indirect(offsets[:]), gates[:], MULT)
-        nc.vector.tensor_tensor(weighted[:, PACK - 2, 0:V], planes[1][PACK - 1][:].indirect(offsets[:, 0 : V // GROUP]), gates[:, 0:V], MULT)
-        nc.vector.tensor_tensor(weighted[:, PACK - 2, V:CUT], last[:, 0, :], gates[:, V:CUT], MULT)
-        nc.vector.tensor_tensor(weighted[:, PACK - 2, CUT:S], last[:, 1, :], gates[:, CUT:S], MULT)
+        for t in range(1, LAST):
+            nc.vector.tensor_tensor(weighted[:, t - 1, :], window(1, t, whole), gates[:], MULT)
+        nc.vector.tensor_tensor(weighted[:, LAST - 1, piece(0)], window(1, LAST, piece(0)), gates[:, piece(0)], MULT)
+        for h in range(HALVES):
+            nc.vector.tensor_tensor(weighted[:, LAST - 1, block(1, h)], shared[:, h, :], gates[:, block(1, h)], MULT)
 
         x_codes = [keep.tile([P, V], U32, name="x_codes%d" % a, align_bytes=64) for a in range(PASSES)]
-        acc = [psum.tile([P, P], F32, name="acc%d" % h, tag=("e2", "x")[h]) for h in range(HALVES)]
+        acc = [psum.tile([P, P], F32, name="acc%d" % h, tag=("bank_a", "bank_b")[h]) for h in range(HALVES)]
 
-        def add_pieces(h):
+        for h in range(HALVES):
             nc.vector.tensor_tensor(
                 sums[1][:, half(h), 1:PACK].rearrange("p (c i) t -> p c t i", i=RUN),
                 weighted[:, :, block(0, h)].rearrange("p t (c i) -> p c t i", i=RUN),
                 weighted[:, :, block(1, h)].rearrange("p t (c i) -> p c t i", i=RUN),
                 ADD,
             )
-
-        def quantize(a, bags):
-            nc.vector.quantize_mx(
-                out=x_codes[a][:, bags].bitcast(FP8X4),
-                scales=x_scale[a][:, bags],
-                in_=sums[a][:, bags, :].rearrange("p v t -> p (v t)"),
-            )
-
-        def multiply(a, h):
-            nc.tensor.matmul_mx(
-                out=acc[h][:],
-                lhsT=w_codes[:, a, :].bitcast(FP8X4),
-                lhsT_scale=w_scale[:, a, :],
-                rhs=x_codes[a][:, half(h)].bitcast(FP8X4),
-                rhs_scale=x_scale[a][:, half(h)],
-                start=(a == 1),
-                stop=(a == 0),
-            )
-
-        for h in range(HALVES):
-            add_pieces(h)
         for h in range(HALVES):
             for a in (1, 0):
-                quantize(a, half(h))
-                multiply(a, h)
+                nc.vector.quantize_mx(
+                    out=x_codes[a][:, half(h)].bitcast(FP8X4),
+                    scales=x_scale[a][:, half(h)],
+                    in_=sums[a][:, half(h), :].rearrange("p v t -> p (v t)"),
+                )
+                nc.tensor.matmul_mx(
+                    out=acc[h][:],
+                    lhsT=w_codes[:, a, :].bitcast(FP8X4),
+                    lhsT_scale=w_scale[:, a, :],
+                    rhs=x_codes[a][:, half(h)].bitcast(FP8X4),
+                    rhs_scale=x_scale[a][:, half(h)],
+                    start=(a == 1),
+                    stop=(a == 0),
+                )
 
         result = [
             keep.tile([P, P], F32, name="result0", tag="sums0", align_bytes=64),

@@ -82,14 +82,14 @@ def tile_picked_bag_lin_relu_sub_l_kernel(tc, xT, w_words, w_scales, b, gate, of
         nc.vector.memset(w_scale[:].rearrange("p a m -> p (a m)").bitcast(U32), 0)
         make_identity(nc, identity[:])
         make_identity(nc, identity_bf16[:])
-        nc.scalar.activation(relu_of_zero[:], zero[:], RELU)
 
         x_rows = xT.rearrange("(a p t) c -> a t p c", a=PASSES, t=PACK)
         nc.sync.dma_start(planes[0][0][:, 0:SYNC_SHARE], x_rows[0, 0][:, 0:SYNC_SHARE])
         nc.scalar.dma_start(planes[0][0][:, SYNC_SHARE:T], x_rows[0, 0][:, SYNC_SHARE:T])
         nc.sync.dma_start(offsets[:], offs)
         gate_blocks = gate.rearrange("d r (h v) -> (d r h) v", h=HALVES)
-        nc.sync.dma_start(gate_rows[0:BLOCKS, :], gate_blocks[0 : (BLOCKS - 1) * (P + 1) + 1 : P + 1, :])
+        nc.scalar.dma_start(gate_rows[0:BLOCKS, :], gate_blocks[0 : (BLOCKS - 1) * (P + 1) + 1 : P + 1, :])
+        nc.scalar.activation(relu_of_zero[:], zero[:], RELU)
         for a, t in [(0, 1), (0, 2), (1, 0), (0, LAST)] + [(1, t) for t in range(1, PACK)]:
             nc.sync.dma_start(planes[a][t][:], x_rows[a, t])
         nc.sync.dma_start(w_codes[:].bitcast(I32), w_words.rearrange("a p m r -> p a (m r)").bitcast(I32))

from contextlib import ExitStack

import concourse.mybir as mybir
from concourse.masks import make_identity

K, T, D, V, N = 1024, 1024, 2, 256, 128
S = D * V
P = 128
PACK = 4
LAST = PACK - 1
PASSES = K // (P * PACK)
HALVES = V // P
BLOCKS = S // P
QUADRANTS = 4
GROUP = 16
CUT = S - P
RUN = 2
SYNC_SHARE = T // 4
FLOPS = 2 * K * V * N

F32 = mybir.dt.float32
BF16 = mybir.dt.bfloat16
I32 = mybir.dt.int32
U32 = mybir.dt.uint32
U16 = mybir.dt.uint16
U8 = mybir.dt.uint8
FP8X4 = mybir.dt.float8_e4m3fn_x4
MULT = mybir.AluOpType.mult
ADD = mybir.AluOpType.add
MAX = mybir.AluOpType.max
COPY = mybir.ActivationFunctionType.Copy
RELU = mybir.ActivationFunctionType.Relu


def tile_picked_bag_lin_relu_sub_l_kernel(tc, xT, w_words, w_scales, b, gate, offs, out):
    nc = tc.nc
    with ExitStack() as ctx:
        keep = ctx.enter_context(tc.tile_pool(name="keep", bufs=1))
        psum = ctx.enter_context(tc.psum_pool(name="psum", bufs=1))

        def plane_tag(a, t):
            return "sums0" if (a, t) == (1, LAST) else "plane%d%d" % (a, t)

        offsets = keep.tile([P, S // GROUP], U16, name="offsets")
        planes = [
            [keep.tile([P, T], F32, name="plane%d%d" % (a, t), tag=plane_tag(a, t), align_bytes=64) for t in range(PACK)]
            for a in range(PASSES)
        ]
        w_codes = keep.tile([P, PASSES, N * PACK], U8, name="w_codes", align_bytes=64)
        w_scale = keep.tile([P, PASSES, N], U8, name="w_scale", align_bytes=64)
        bias = keep.tile([P, 1], F32, name="bias")
        identity = keep.tile([P, P], F32, name="identity")
        identity_bf16 = keep.tile([P, P], BF16, name="identity_bf16")
        zero = keep.tile([P, 1], F32, name="zero")
        relu_of_zero = keep.tile([P, 1], F32, name="relu_of_zero")

        gate_rows = keep.tile([P, P], F32, name="gate_rows")
        gate_cols = keep.tile([P, BLOCKS], F32, name="gate_cols")
        gate_cols_psum = psum.tile([P, P], F32, name="gate_cols_psum", tag="bank_a")
        gates_psum = [psum.tile([P, V], BF16, name="gates_psum%d" % d, tag=("bank_c", "bank_b")[d]) for d in range(D)]
        gate_cols_bf16 = keep.tile([P, BLOCKS], BF16, name="gate_cols_bf16")

        sums = [keep.tile([P, V, PACK], BF16, name="sums%d" % a, tag="sums%d" % a, align_bytes=64) for a in range(PASSES)]
        x_scale = [keep.tile([P, V], U8, name="x_scale%d" % a, align_bytes=64) for a in range(PASSES)]

        def half(h):
            return slice(h * P, (h + 1) * P)

        def piece(d):
            return slice(d * V, (d + 1) * V)

        def block(d, h):
            return half(HALVES * d + h)

        def window(a, t, entries):
            return planes[a][t][:].indirect(offsets[:, entries.start // GROUP : entries.stop // GROUP])

        whole = slice(0, S)

        nc.gpsimd.memset(gate_rows[:], 0.0)
        nc.vector.memset(zero[:], 0.0)
        nc.vector.memset(w_scale[:].rearrange("p a m -> p (a m)").bitcast(U32), 0)
        make_identity(nc, identity[:])
        make_identity(nc, identity_bf16[:])

        x_rows = xT.rearrange("(a p t) c -> a t p c", a=PASSES, t=PACK)
        nc.sync.dma_start(planes[0][0][:, 0:SYNC_SHARE], x_rows[0, 0][:, 0:SYNC_SHARE])
        nc.scalar.dma_start(planes[0][0][:, SYNC_SHARE:T], x_rows[0, 0][:, SYNC_SHARE:T])
        nc.sync.dma_start(offsets[:], offs)
        gate_blocks = gate.rearrange("d r (h v) -> (d r h) v", h=HALVES)
        nc.scalar.dma_start(gate_rows[0:BLOCKS, :], gate_blocks[0 : (BLOCKS - 1) * (P + 1) + 1 : P + 1, :])
        nc.scalar.activation(relu_of_zero[:], zero[:], RELU)
        for a, t in [(0, 1), (0, 2), (1, 0), (0, LAST)] + [(1, t) for t in range(1, PACK)]:
            nc.sync.dma_start(planes[a][t][:], x_rows[a, t])
        nc.sync.dma_start(w_codes[:].bitcast(I32), w_words.rearrange("a p m r -> p a (m r)").bitcast(I32))
        for q in range(QUADRANTS):
            nc.sync.dma_start(
                w_scale[32 * q : 32 * q + 4, :, :].bitcast(I32),
                w_scales[:, 4 * q : 4 * q + 4, :].rearrange("a q m -> q a m").bitcast(I32),
            )
        nc.sync.dma_start(bias[:], b)

        def add_turned(total, parts):
            for d in range(D):
                nc.tensor.matmul(total, parts[d], identity[:], start=(d == 0), stop=(d == D - 1), is_transpose=True)

        nc.tensor.transpose(gate_cols_psum[:], gate_rows[:], identity[:])
        nc.scalar.copy(gate_cols_bf16[:], gate_cols_psum[:, 0:BLOCKS])
        nc.scalar.copy(gate_cols[:], gate_cols_psum[:, 0:BLOCKS])

        def turn(picked, t, tag):
            bank = psum.tile([P, HALVES, D, P], BF16, name="entries%d" % t, tag=tag)
            for h in range(HALVES):
                for d in range(D):
                    nc.tensor.transpose(bank[:, h, d, :], picked[:, block(d, h)], identity_bf16[:])
            return bank

        def gather(t, tag):
            picked = keep.tile([P, S], BF16, name="picked%d" % t, tag="picked%d" % t)
            nc.vector.tensor_copy(picked[:], window(0, t, whole))
            return turn(picked, t, tag)

        def scale(product, turned, d, h):
            j = HALVES * d + h
            nc.scalar.activation(product, turned, COPY, scale=gate_cols[:, j : j + 1])

        def scale_and_sum(bank, t):
            for h in range(HALVES):
                scaled = keep.tile([P, D, P], F32, name="scaled%d%d" % (t, h), tag="scaled%d%d" % (t, h))
                for d in range(D):
                    scale(scaled[:, d, :], bank[:, h, d, :], d, h)
                add_turned(summed0[h][:, t, :], [scaled[:, d, :] for d in range(D)])

        summed0 = [psum.tile([P, PACK, P], F32, name="summed0%d" % h) for h in range(HALVES)]

        picked0 = keep.tile([P, S], BF16, name="picked0")
        nc.vector.tensor_copy(picked0[:, piece(0)], window(0, 0, piece(0)))
        nc.scalar.activation(picked0[:, piece(1)], window(0, 0, piece(1)), COPY)
        gates = keep.tile([P, S], F32, name="gates")
        for d in range(D):
            for h in range(HALVES):
                j = HALVES * d + h
                column = gate_cols_bf16[:, j : j + 1].to_broadcast([P, P])
                nc.tensor.transpose(gates_psum[d][:, half(h)], column, identity_bf16[:])
            nc.scalar.copy(gates[:, piece(d)], gates_psum[d][:])
        bank0 = turn(picked0, 0, "bank_a")
        bank1 = gather(1, "bank_c")
        scale_and_sum(bank0, 0)
        bank2 = gather(2, "bank_a")

        first_products = keep.tile([P, S], F32, name="first_products")
        for entries in (piece(0), slice(V, CUT), slice(CUT, S)):
            nc.vector.tensor_tensor(first_products[:, entries], window(1, 0, entries), gates[:, entries], MULT)
        for h in range(HALVES):
            nc.vector.tensor_tensor(
                sums[1][:, half(h), 0], first_products[:, block(0, h)], first_products[:, block(1, h)], ADD
            )
        scale_and_sum(bank1, 1)

        picked3 = keep.tile([P, S], BF16, name="picked3", tag="picked1")
        banks3 = [
            psum.tile([P, HALVES, P], BF16, name="entries3%d" % d, tag=("bank_c", "bank_b")[d]) for d in range(D)
        ]
        for d in range(D):
            nc.scalar.activation(picked3[:, piece(d)], window(0, LAST, piece(d)), COPY)
            for h in range(HALVES):
                nc.tensor.transpose(banks3[d][:, h, :], picked3[:, block(d, h)], identity_bf16[:])
        scale_and_sum(bank2, 2)
        scaled3 = [keep.tile([P, D, P], F32, name="scaled3%d" % h) for h in range(HALVES)]
        for d in range(D):
            for h in range(HALVES):
                scale(scaled3[h][:, d, :], banks3[d][:, h, :], d, h)
        for h in range(HALVES):
            add_turned(summed0[h][:, LAST, :], [scaled3[h][:, d, :] for d in range(D)])

        weighted = keep.tile([P, PACK - 1, S], F32, name="weighted", tag="scaled10")
        shared = keep.tile([P, HALVES, P], F32, name="shared", tag="picked1")
        for h in range(HALVES):
            nc.scalar.activation(shared[:, h, :], window(1, LAST, block(1, h)), COPY)
        for h in range(HALVES):
            nc.scalar.copy(sums[0][:, half(h), :], summed0[h][:].rearrange("p t v -> p v t"))

        for t in range(1, LAST):
            nc.vector.tensor_tensor(weighted[:, t - 1, :], window(1, t, whole), gates[:], MULT)
        nc.vector.tensor_tensor(weighted[:, LAST - 1, piece(0)], window(1, LAST, piece(0)), gates[:, piece(0)], MULT)
        for h in range(HALVES):
            nc.vector.tensor_tensor(weighted[:, LAST - 1, block(1, h)], shared[:, h, :], gates[:, block(1, h)], MULT)

        x_codes = [keep.tile([P, V], U32, name="x_codes%d" % a, align_bytes=64) for a in range(PASSES)]
        acc = [psum.tile([P, P], F32, name="acc%d" % h, tag=("bank_a", "bank_b")[h]) for h in range(HALVES)]

        for h in range(HALVES):
            nc.vector.tensor_tensor(
                sums[1][:, half(h), 1:PACK].rearrange("p (c i) t -> p c t i", i=RUN),
                weighted[:, :, block(0, h)].rearrange("p t (c i) -> p c t i", i=RUN),
                weighted[:, :, block(1, h)].rearrange("p t (c i) -> p c t i", i=RUN),
                ADD,
            )
        for h in range(HALVES):
            for a in (1, 0):
                nc.vector.quantize_mx(
                    out=x_codes[a][:, half(h)].bitcast(FP8X4),
                    scales=x_scale[a][:, half(h)],
                    in_=sums[a][:, half(h), :].rearrange("p v t -> p (v t)"),
                )
                nc.tensor.matmul_mx(
                    out=acc[h][:],
                    lhsT=w_codes[:, a, :].bitcast(FP8X4),
                    lhsT_scale=w_scale[:, a, :],
                    rhs=x_codes[a][:, half(h)].bitcast(FP8X4),
                    rhs_scale=x_scale[a][:, half(h)],
                    start=(a == 1),
                    stop=(a == 0),
                )

        result = [
            keep.tile([P, P], F32, name="result0", tag="sums0", align_bytes=64),
            keep.tile([P, P], F32, name="result1"),
        ]
        nc.vector.tensor_scalar(result[0][:], acc[0][:], bias[:], 0.0, ADD, MAX)
        nc.sync.dma_start(out[:, half(0)], result[0][:])
        nc.scalar.activation(result[1][:], acc[1][:], RELU, bias=bias[:])
        nc.scalar.dma_start(out[:, half(1)], result[1][:])
